import numpy as np, ml_dtypes
CORES = [48,51,52,55]
N = 4
import mx_ref
BF = ml_dtypes.bfloat16
def pick(q, e):
    c = np.concatenate([q[0].reshape(128, -1, 4), np.zeros((128, 1, 4), np.uint8)], axis=1); s = np.concatenate([q[1], np.ones((16, 1), np.uint8)], axis=1)
    return (np.ascontiguousarray(c[:, e].reshape(128, -1)), np.ascontiguousarray(s[:, e]))
def join(*qs):
    return (np.concatenate([q[0] for q in qs], axis=1), np.concatenate([q[1] for q in qs], axis=1))
def put(q, e, v):
    c, s = q[0].reshape(128, -1, 4).copy(), q[1].copy(); c[:, e] = v[0].reshape(128, -1, 4); s[:, e] = v[1]
    return (c.reshape(128, -1), s)
def pk(c, s):
    return (np.ascontiguousarray(c), mx_ref.live(s))
def emit(q):
    return q[0], q[1]
def decode(q):
    o = []
    for b in range(4):
        e = np.zeros((128, 128, 4), np.float32); e[np.arange(128), np.arange(128), b] = 1
        o.append(mx_ref.matmul(mx_ref.quantize(e.reshape(128, 512).astype(BF)), q))
    return np.stack(o, axis=2).reshape(128, -1)
def f(rng, *shape):
    return mx_ref.flush((rng.standard_normal(shape, dtype=np.float32) * np.exp2(rng.integers(-2, 3, shape[:-1] + (1,)))).astype(BF))
def wide(rng, *shape, cols=0):
    v = rng.standard_normal(shape, dtype=np.float32) * np.exp2(rng.integers(-12, 13, shape)).astype(np.float32)
    if cols: v *= np.repeat(np.exp2(rng.integers(-cols, cols + 1, shape[:-2] + (1, shape[-1] // 4))) * (rng.random(shape[:-2] + (1, shape[-1] // 4)) > 0.0625), 4, axis=-1).astype(np.float32)
    return mx_ref.flush(v.astype(BF))
T, CAPP = 192, 48
def quads(q, e):
    c = np.concatenate([q[0].reshape(128, -1, 4), np.zeros((128, 1, 4), np.uint8)], axis=1); s = np.concatenate([q[1], np.ones((16, 1), np.uint8)], axis=1)
    return (np.concatenate([c[32 * h:32 * h + 32][:, e[h]] for h in range(4)]).reshape(128, -1), np.concatenate([s[4 * h:4 * h + 4][:, e[h]] for h in range(4)]))
def level(b, z):
    n, e = z[1].shape[1], []
    for h in range(4):
        only = np.where(np.arange(4)[:, None] == h, np.arange(n)[None, :], -1)
        e.append(np.argmax(mx_ref.matmul(b, quads(z, only)) + np.float32(0), axis=0))
    e = np.stack(e)
    return e, quads(b, e)
def big(v):
    v = v.astype(np.float32)
    v[np.abs(v) < np.float32(2.0 ** -16)] = 0
    return v.astype(BF)
def coarse(v):
    v = v.copy()
    v[:, N:] = 0
    return np.stack([v.reshape(128, 512)] * N)
def planted(rng, cell, low=False):
    at = rng.permutation(N)[np.arange(128) // (128 // N)]
    c = (1 + rng.random((128, 128, 4))) * (at[:, None] == np.arange(128)[None, :])[:, :, None]
    on = at[None, :, None] == cell[:, None, :]
    v = np.where(on[:, :, :, None], 8 + 8 * rng.random((N, 128, T, 4)), 2 * rng.random((N, 128, T, 4)) - 1)
    if low:
        u = 1 + rng.random((N, 128, T // 2, 4))
        v[:, :, 1::2] = np.where(on[:, :, 1::2, None], -0.5 * u, -8 * u)
        c = c * 2.0 ** 20
    v = v * np.exp2(rng.integers(-3, 4, (N, 1, T, 1)))
    return {"x": big(v.reshape(N, 128, 4 * T)), "co": coarse(big(c))}
def setup_inputs(rng):
    return {"x": big(f(rng, N, 128, 4 * T)), "co": coarse(big(f(rng, 128, 512)).reshape(128, 128, 4)), "b1": big(f(rng, N, 128, 512)), "b2": big(f(rng, N, 128, 512)), "w": f(rng, N, 128, 512)}
def setup_inputs_spread(rng):
    d = setup_inputs(rng)
    d["x"], d["b1"] = big(wide(rng, N, 128, 4 * T, cols=6)), big(wide(rng, N, 128, 512))
    return d
def setup_inputs_ties(rng):
    d = setup_inputs(rng)
    for k in ("b1", "b2"):
        b = d[k].reshape(N, 128, 128, 4).copy()
        for r in range(N):
            for h in range(4): b[r, 32 * h:32 * h + 32] = b[r, 32 * h:32 * h + 32][:, rng.permutation(128) % 32]
        d[k] = b.reshape(N, 128, 512)
    c = d["co"][0].reshape(128, 128, 4).copy()
    c[:, :N] = c[:, rng.permutation(N) % (N // 2)]
    d["co"] = coarse(c)
    return d
def setup_inputs_crowd(rng):
    g, cell = int(rng.integers(0, N)), []
    for s in range(N):
        o = rng.permutation(np.delete(np.arange(N), g))
        if o[0] == s: o = o[::-1]
        m = int(rng.integers(1, 17))
        cell.append(rng.permutation(np.concatenate([np.full(CAPP + m, g), np.full(CAPP, o[0]), o[1:][rng.integers(0, N - 2, T - 2 * CAPP - m)]])))
    return {**setup_inputs(rng), **planted(rng, np.stack(cell))}
def setup_inputs_few(rng):
    g, a, b = [int(i) for i in rng.permutation(N)[:3]]
    cell = np.delete(np.arange(N), g)[rng.integers(0, N - 1, (N, T))]
    cell[a], cell[b] = a, a
    return {**setup_inputs(rng), **planted(rng, cell, low=True)}
def setup_inputs_zero(rng):
    d, h = setup_inputs(rng), [int(i) for i in rng.permutation(4)]
    neg, pat, gap = [slice(32 * i, 32 * i + 32) for i in h[:3]]
    p = (1 + rng.random((32, 1, 4))) * np.exp2(rng.integers(-2, 3, (32, 1, 1)))
    v, b, c = d["x"].astype(np.float32).reshape(N, 128, T, 4), d["b1"].astype(np.float32).reshape(N, 128, 128, 4), d["co"][0].reshape(128, 128, 4).copy()
    u = d["b2"].astype(np.float32)
    c[neg], c[pat] = 0, 0
    c[:, int(rng.integers(0, N))] = 0
    v[:, neg], b[:, neg], u[:, neg] = -np.abs(v[:, neg]), np.abs(b[:, neg]), np.abs(u[:, neg])
    v[:, pat] = p
    for r in range(N):
        e, k = rng.permutation(T), rng.integers(0, 4, 128)
        v[r, gap][:, e[T // 8:T // 2]] = 0
        v[r][:, e[:T // 8]] = 0
        k[int(rng.integers(0, 128))] = 0
        b[r, pat] = p * np.exp2(-k.astype(np.float64))[:, None]
        if r % 2 == 0: b[r, neg, int(rng.integers(0, 128))] = 0
    k = np.float32(2.0 ** 20)
    d["x"], d["b1"], d["b2"], d["co"] = big(v.reshape(N, 128, 4 * T) * k), big(b.reshape(N, 128, 512) * k), big(u * k), coarse(c)
    return d
def check_inputs(d):
    b = []
    for k in ("x", "co", "b1", "b2", "w"):
        v = np.abs(d[k].astype(np.float32))
        if not (np.isfinite(v).all() and ((v == 0) | (v >= 2.0 ** -30) & (v <= 2.0 ** 30)).all()): b.append("a value of " + k)
    c = d["co"].astype(np.float32)
    if (c[:, :, 4 * N:] != 0).any(): b.append("co has numbers behind its first N columns")
    if (c != c[:1]).any(): b.append("co isn't the same on all ranks")
    return b
def reference(x, co, b1, b2, w):
    oc, osc = np.zeros((N, 128, 8 * T), np.uint8), np.zeros((N, 16, 2 * T), np.uint8)
    wn, y = np.full((N, 8, T), -1, np.float32), np.zeros((N, 128, T), np.float32)
    q = [mx_ref.quantize(x[s]) for s in range(N)]
    taken = np.full((N, N, CAPP), -1)
    for s in range(N):
        cell = np.argmax(mx_ref.matmul(mx_ref.quantize(co[s]), q[s])[:N] + np.float32(0), axis=0)
        for d in range(N):
            t = np.flatnonzero(cell == d)[:CAPP]
            taken[s, d, :len(t)] = t
    home = [pick(q[s], np.full(2 * T, -1)) for s in range(N)]
    for d in range(N):
        z = join(*[pick(q[s], taken[s, d]) for s in range(N)])
        n1, v1 = level(mx_ref.quantize(b1[d]), z)
        r = mx_ref.quantize((decode(z) - decode(v1)).astype(BF))
        n2, v2 = level(mx_ref.quantize(b2[d]), r)
        for s in range(N):
            k = np.flatnonzero(taken[s, d] >= 0)
            t, i = taken[s, d][k], s * CAPP + k
            wn[s, :4, t], wn[s, 4:, t] = n1[:, i].T, n2[:, i].T
            home[s] = put(put(home[s], t, pick(v1, i)), T + t, pick(v2, i))
    for s in range(N):
        oc[s], osc[s] = emit(home[s])
        m = mx_ref.matmul(mx_ref.quantize(w[s]), home[s])
        y[s] = m[:, :T] + m[:, T:]
    return {"oc": oc, "osc": osc, "wn": wn, "y": y}

@@ -1,0 +1,356 @@
+from concourse.bass import DstId, RemoteDMATransfer
+from concourse.mybir import dt, AluOpType, AxisListType, ActivationFunctionType
+
+A = AluOpType
+F = ActivationFunctionType
+TOK, CAP, NR = 192, 48, 4
+LOW = -1e29
+RND = 1.5 * 2.0 ** 27
+
+
+def _codes(n):
+    return ("sbuf", [128, n], "float8_e4m3fn_x4")
+
+
+def _plane(n):
+    return ("sbuf", [128, n], "uint8")
+
+
+def _sb(n, d):
+    return ("sbuf", [128, n], d)
+
+
+SCRATCH = {}
+for _n, _w in (("xq", 192), ("cq", 128), ("wq", 128), ("b1q", 512), ("b2q", 512), ("trq", 256), ("wlq", 128), ("epq", 512), ("enq", 512),
+               ("otq", 128), ("abq", 140), ("xtq", 140), ("zsq", 144), ("zq", 192), ("vbq", 192), ("lvq", 208), ("v2q", 144), ("lwq", 208),
+               ("rq", 192), ("o1q", 192), ("o2q", 192)):
+    SCRATCH[_n] = _codes(_w)
+    SCRATCH[_n + "s"] = _plane(_w)
+for _n, _w in (("xb", 768), ("cb", 512), ("wb", 512), ("bm1", 2048), ("bm2", 2048), ("trb", 1024), ("wlb", 512), ("epb", 520), ("enb", 520),
+               ("ot", 512), ("ab", 560), ("xt", 560), ("rt", 768), ("zz", 512), ("on1", 520), ("t1", 128), ("im", 128), ("zr", 256),
+               ("jk1", 1024), ("jk2", 1024), ("nbf", 16), ("ln", 128), ("tr", 128)):
+    SCRATCH[_n] = _sb(_w, "bfloat16")
+for _n, _w in (("rma", 16), ("ua", 16), ("r2", 2), ("hc", 2), ("nl", 2), ("tk", 4), ("ib", 12), ("ibc", 12), ("vl", 1), ("hcol", 1),
+               ("df", 1), ("e0", 1), ("e4", 1), ("off", 6), ("rm1", 1024), ("rm2", 1024), ("nf", 16), ("pt0", 24), ("pt1", 24), ("pt2", 24),
+               ("tf", 2), ("q1", 2), ("q2", 2), ("pf", 2), ("wt", 208), ("wno", 192), ("ysb", 192)):
+    SCRATCH[_n] = _sb(_w, "float32")
+for _n, _w in (("pi", 1), ("pa", 1), ("pb", 1), ("gi", 1), ("ui", 1), ("ti", 1), ("hi", 1), ("ofi", 6), ("ofj", 6), ("vi", 2), ("ai", 2), ("bi", 2)):
+    SCRATCH[_n] = _sb(_w, "int32")
+for _n, _w in (("zl", 12), ("zl2", 4), ("pl", 12), ("l1", 12), ("l2", 12), ("l2b", 4), ("offl", 6), ("offp", 6)):
+    SCRATCH[_n] = _sb(_w, "uint16")
+for _n in ("psa", "psb", "psc", "psd", "pd0", "pd1", "pd2", "pd3"):
+    SCRATCH[_n] = ("psum", [128, 512], "float32")
+SEMAPHORES = ["qv", "qs", "qt", "qg", "dx", "dco", "db1", "db2", "dw", "dz", "dv", "st", "zin", "vin", "win", "nin", "left"]
+
+
+def _mask(topo, src, peers):
+    out, far, near = {}, 0, 0
+    for c in peers:
+        e = topo.engines(src, c)
+        if topo.die(src) != topo.die(c):
+            pick = e[far * 8:far * 8 + 8:2]
+            far += 1
+        else:
+            pick = e[1 + near * 8:9 + near * 8:2]
+            near += 1
+        out[c] = pick
+    return out
+
+
+def rank_program(g, core, T, topo):
+    rank = T.rank_of(core)
+    if rank is None:
+        return
+    S = T.sem
+    eng = {"v": g.vector, "s": g.scalar, "t": g.tensor, "g": g, "y": g.sync}
+    qsem = {"v": "qv", "s": "qs", "t": "qt", "g": "qg"}
+    cnt = {"v": 0, "s": 0, "t": 0, "g": 0}
+    seen = {q: {} for q in eng}
+
+    def need(q, *deps):
+        for sem, val in deps:
+            if seen[q].get(sem, 0) < val:
+                eng[q].wait_ge(S[sem], val)
+                seen[q][sem] = val
+
+    def done(q, ins):
+        ins.then_inc(S[qsem[q]], 1)
+        cnt[q] += 1
+        return (qsem[q], cnt[q])
+
+    V, SC, TE = g.vector, g.scalar, g.tensor
+    stores = [0]
+
+    def dma(q, out, in_, sem):
+        eng[q].dma_start(out, in_).then_inc(S[sem], 16)
+        if sem == "st":
+            stores[0] += 1
+
+    def ts(out, in0, s1, s2, op0, op1, *deps):
+        need("v", *deps)
+        if op1 is None:
+            return done("v", V.tensor_scalar(out, in0, s1, s2, op0))
+        return done("v", V.tensor_scalar(out, in0, s1, s2, op0, op1))
+
+    def tt(out, a, b, op, *deps):
+        need("v", *deps)
+        return done("v", V.tensor_tensor(out, a, b, op))
+
+    def fill(ap, c, *deps):
+        need("v", *deps)
+        return done("v", V.memset(ap, c))
+
+    def copy(out, in_, *deps):
+        need("v", *deps)
+        return done("v", V.tensor_copy(out, in_))
+
+    def quant(q, s, in_, *deps):
+        need("v", *deps)
+        return done("v", V.quantize_mx(q, s, in_))
+
+    def act(out, in_, func, *deps):
+        need("s", *deps)
+        return done("s", SC.activation(out, in_, func))
+
+    def mm(out, name, c0, c1, mov, m0, m1, start, stop, *deps):
+        need("t", *deps)
+        return done("t", TE.matmul_mx(out, T[name][:, c0:c1], T[name + "s"][:, c0:c1], T[mov][:, m0:m1], T[mov + "s"][:, m0:m1], start, stop))
+
+    def pick(dst, d0, d1, win, w1, lst, *deps):
+        need("v", *deps)
+        need("s", *deps)
+        cv = done("v", V.tensor_copy(T[dst][:, d0:d1].bitcast(dt.uint32), T[win][:, 0:w1].bitcast(dt.uint32).indirect(lst)))
+        cs = done("s", SC.activation(T[dst + "s"][:, d0:d1], T[win + "s"][:, 0:w1].indirect(lst), F.Copy))
+        return cv, cs
+
+    peers = [T.cores[(rank + 1 + a) % NR] for a in range(3)]
+    emask = _mask(topo, core, peers)
+    landing = sum(len(_mask(topo, c, [T.cores[(T.rank_of(c) + 1 + a) % NR] for a in range(3)])[core]) for c in peers)
+    left = [0]
+
+    def fan(srcs, dsts, sem, *deps):
+        need("g", *deps)
+        tr = []
+        for a, c in enumerate(peers):
+            rid, pid, _ = topo.addr(c)
+            tr.append(RemoteDMATransfer(dst_ids=[DstId(rid=rid, pnc=pid)], dma_engine_mask=sum(1 << e for e in emask[c]),
+                                        remote_sem=S[sem], srcs=[srcs[a]], dsts=[dsts[a]]))
+            left[0] += len(emask[c])
+        g.remote_dma_fused(tr, local_sem=S["left"])
+
+    dma("y", T.xb[:], T.x[:], "dx")
+    dma("s", T.cb[:], T.co[:], "dco")
+
+    c_pi = done("g", g.iota(T.pi[:], [[0, 1]], 0, 1))
+    c_im = done("g", g.iota(T.im[:], [[0, 8], [1, 16]], 0, 0, allow_small_or_imprecise_dtypes=True))
+    c_ib = done("g", g.iota(T.ib[:], [[256, 4], [16, 3]], 1024, 0, allow_small_or_imprecise_dtypes=True))
+    c_zz = fill(T.zz[:], 0.0)
+    c_on = fill(T.on1[:], 1.0)
+    c_tr = fill(T.trb[:], 1.0)
+    c_tr = fill(T.trb[:, 1:512:4], 0.0, c_tr)
+    c_ot = fill(T.ot[:], 0.0)
+    c_zr = fill(T.zr[:], 0.0)
+    c_rm = fill(T.rma[:], LOW)
+    c_ln = fill(T.ln[:], 0.0)
+    c_zr = fill(T.zr[:, 128:129], LOW, c_zr)
+    for d in range(NR):
+        rel = (d - rank - 1) % NR
+        if rel:
+            c_ot = fill(T.ot[:, 3 + 4 * d:4 + 4 * d], 2.0 * rel, c_ot)
+    for k, b in enumerate(("bm1", "bm2")):
+        for h in range(4):
+            c_z = act(T[b][:, 512 * h:512 * h + 512], T.zz[:], F.Copy, c_zz)
+        need("y", c_z)
+        for h in range(4):
+            dma("y", T[b][32 * h:32 * h + 32, 512 * h:512 * h + 512], (T.b1, T.b2)[k][32 * h:32 * h + 32, :], ("db1", "db2")[k])
+    dma("y", T.wb[:], T.w[:], "dw")
+    need("g", c_on)
+    c_t1 = done("g", g.affine_select(T.t1[:], T.on1[:, 0:128], [[1, 128]], A.is_gt, 0.0, 0, -1))
+    need("g", c_t1, c_tr)
+    done("g", g.affine_select(T.trb[:, 0:512:4], T.t1[:], [[1, 128]], A.not_equal, 1024.0, 0, -1))
+    c_tri = done("g", g.affine_select(T.trb[:, 513:1024:4], T.t1[:], [[1, 128]], A.not_equal, 1024.0, 0, -1))
+    c_ep = done("g", g.affine_select(T.epb[:], T.on1[:], [[1, 520]], A.is_equal, 0.0, -4, -4))
+    need("s", c_ep)
+    c_en = done("s", SC.activation(T.enb[:], T.epb[:], F.Copy, scale=-1.0))
+    ts(T.pa[:], T.pi[:], 112, None, A.bitwise_and, None, c_pi)
+    ts(T.pb[:], T.pi[:], 15, None, A.bitwise_and, None)
+    c_vl = ts(T.vl[:], T.pi[:], 64.0, None, A.is_ge, None)
+    ts(T.gi[:], T.pi[:], 4, None, A.arith_shift_right, None)
+    ts(T.ui[:], T.pi[:], 2, 3, A.arith_shift_right, A.bitwise_and)
+    ts(T.ti[:], T.pi[:], 3, None, A.bitwise_and, None)
+    c_h = ts(T.hi[:], T.pi[:], 5, None, A.arith_shift_right, None)
+    copy(T.tk[:, 0:1], T.pa[:], c_vl)
+    copy(T.tk[:, 1:2], T.pb[:])
+    ts(T.tk[:, 2:3], T.pa[:], 64.0, T.vl[:], A.add, A.mult)
+    c_tk = ts(T.tk[:, 3:4], T.pb[:], T.vl[:], None, A.mult, None)
+    c_ib = ts(T.ibc[:], T.ib[:], RND, None, A.add, None, c_ib)
+    c_df = tt(T.df[:], T.gi[:], T.ui[:], A.subtract, c_h)
+    c_hc = ts(T.hcol[:], T.hi[:], 128.0, None, A.mult, None)
+
+    c_q = quant(T.cq[:], T.cqs[:], T.cb[:], ("dco", 16))
+    quant(T.trq[:], T.trqs[:], T.trb[:], c_tri)
+    c_x = quant(T.xq[:], T.xqs[:], T.xb[:], ("dx", 16))
+    need("y", c_q)
+    for b in ("lvq", "lwq"):
+        dma("y", T[b][:, 192:208].bitcast(dt.uint8), T.cq[:, 64:80].bitcast(dt.uint8), "dz")
+        dma("y", T[b + "s"][:, 192:208], T.cqs[:, 64:80], "dz")
+    m0 = mm(T.psa[:, 0:128], "xq", 0, 128, "cq", 0, 128, True, True, c_x)
+    m1 = mm(T.psb[:, 0:128], "xq", 64, 192, "cq", 0, 128, True, True)
+
+    def scan(out, d0, d1, *deps):
+        need("v", *deps)
+        return done("v", V.tensor_tensor_scan(out, d0, d1, LOW, A.add, A.max))
+    s0 = scan(T.rma[:, 1:5], T.zz[:, 0:4], T.psa[:, 0:4], m0, c_rm)
+    s1 = scan(T.rma[:, 9:13], T.zz[:, 0:4], T.psb[:, 0:4], m1)
+    u0 = ts(T.ua[:, 0:5], T.rma[:, 0:5], T.rma[:, 4:5], None, A.is_equal, None, s0)
+    u1 = ts(T.ua[:, 8:13], T.rma[:, 8:13], T.rma[:, 12:13], T.vl[:], A.is_equal, A.mult, s1)
+    tt(T.ot[:, 0:16:4], T.ua[:, 1:5], T.ua[:, 0:4], A.subtract, u0)
+    o1 = tt(T.ot[:, 1:16:4], T.ua[:, 9:13], T.ua[:, 8:12], A.subtract, u1)
+    c_o = quant(T.otq[:], T.otqs[:], T.ot[:], o1)
+    m0 = mm(T.psc[:, 0:128], "trq", 0, 128, "otq", 0, 128, True, True, c_o)
+    m1 = mm(T.psd[:, 0:128], "trq", 128, 256, "otq", 0, 128, True, True)
+    need("v", m0)
+    done("v", V.tensor_reduce(T.r2[:, 0:1], T.psc[:, 0:4], AxisListType.X, A.max))
+    need("v", m1)
+    r = done("v", V.tensor_reduce(T.r2[:, 1:2], T.psd[:, 0:4], AxisListType.X, A.max))
+    c_hcv = ts(T.hc[:], T.r2[:], -7.5, RND, A.add, A.add, r)
+    c_nl = []
+    for s in range(2):
+        c_nl.append(ts(T.nl[:, s:s + 1], T.hc[:, s:s + 1], RND, T.r2[:, s:s + 1], A.subtract, A.subtract, c_hcv))
+    for t in range(4):
+        ts(T.ab[:, 512 + t:560:4], T.ibc[:], T.hc[:, t // 2:t // 2 + 1], T.tk[:, t:t + 1], A.is_equal, A.mult)
+    for t in range(4):
+        c_a = ts(T.ab[:, t:512:4], T.im[:], T.nl[:, t // 2:t // 2 + 1], 0.0, A.add, A.is_equal, c_nl[t // 2], c_im)
+    c_a = quant(T.abq[:], T.abqs[:], T.ab[:], c_a)
+    m0 = mm(T.psa[:, 0:128], "abq", 0, 128, "abq", 12, 140, True, True, c_a)
+    c_l = copy(T.zl[:, 0:9], T.psa[:, 116:125], m0)
+    zv, zs = pick("zsq", 0, 144, "xq", 192, T.zl[:, 0:9], c_l)
+    fan([T.zsq[:, 48 * a:48 * a + 48].bitcast(dt.uint8) for a in range(3)], [T.zq[:, 48 * (2 - a):48 * (2 - a) + 48].bitcast(dt.uint8) for a in range(3)], "zin", zv)
+    fan([T.zsqs[:, 48 * a:48 * a + 48] for a in range(3)], [T.zqs[:, 48 * (2 - a):48 * (2 - a) + 48] for a in range(3)], "zin", zs)
+    c_l = copy(T.zl2[:, 0:3], T.psa[:, 125:128])
+    zo = pick("zq", 144, 192, "xq", 192, T.zl2[:, 0:3], c_l)
+
+    c_b1 = quant(T.b1q[:], T.b1qs[:], T.bm1[:], ("db1", 64))
+    for b in range(4):
+        c_e = quant(T.epq[:, 128 * b:128 * b + 128], T.epqs[:, 128 * b:128 * b + 128], T.epb[:, 4 - b:516 - b], c_ep)
+    c_w = fill(T.wlb[:], 0.0)
+    c_e0 = ts(T.e0[:], T.df[:], 0.0, None, A.is_equal, None)
+    c_e4 = ts(T.e4[:], T.df[:], 4.0, None, A.is_equal, None)
+    for t in range(4):
+        c_w = ts(T.wlb[:, 129 * t:128 * t + 128:4], T.im[:, 0:32], T.tk[:, 1:2], None, A.is_equal, None, c_w)
+    for k, (c, e) in enumerate(((-16., T.e0), (-16., T.e4), (-12., T.e4), (-8., T.e0), (-8., T.e4), (-4., T.e4))):
+        c_f = ts(T.off[:, k:k + 1], T.ti[:], c, e[:], A.add, A.mult, c_e4)
+    c_w = quant(T.wlq[:], T.wlqs[:], T.wlb[:], c_w)
+    c_ol = ts(T.offl[:], T.off[:], 16.0, None, A.add, None, c_f)
+    c_oi = ts(T.ofi[:], T.off[:], 16.0, None, A.add, None)
+    for b in range(4):
+        c_n = quant(T.enq[:, 128 * b:128 * b + 128], T.enqs[:, 128 * b:128 * b + 128], T.enb[:, 4 - b:516 - b], c_en)
+    fill(T.xt[:, 96:560], 0.0)
+    for p in (T.pt0, T.pt1, T.pt2):
+        fill(p[:], 0.0)
+    c_b2 = quant(T.b2q[:], T.b2qs[:], T.bm2[:], ("db2", 64))
+
+    banks = ("psa", "psb", "psc", "psd")
+
+    def scores(tok, book, *deps):
+        return [mm(T[banks[k]][:, 0:256], tok, 64 * (k // 2), 64 * (k // 2) + 128, book, 256 * (k % 2), 256 * (k % 2) + 256, True, True, *deps)
+                for k in range(4)]
+
+    def words(ms, rm, jk, base, pt):
+        for k in range(4):
+            c = scan(rm[:, 256 * k:256 * k + 256], T.zr[:], T[banks[k]][:, 0:256], ms[k])
+            for h in range(2):
+                a = 256 * k + 128 * h
+                need("s", c)
+                cs = done("s", SC.activation(jk[:, a:a + 128], rm[:, a:a + 128], F.Sign, bias=rm[:, a + 127:a + 128], scale=-1.0,
+                                             accum_out=T.nf[:, base + 2 * k + h:base + 2 * k + h + 1]))
+        c1 = ts(pt[:, 0:8], T.nf[:, base:base + 8], RND, RND, A.add, A.subtract, cs)
+        c1 = tt(pt[:, 8:16], T.nf[:, base:base + 8], pt[:, 0:8], A.subtract, c1)
+        return cs, c1
+
+    def tolist(pt, off, bank, c1):
+        need("v", c1)
+        c = done("v", V.tensor_copy(T.xt[:, 0:96], pt[:, 0:24].indirect(off[:, 0:6])))
+        c = quant(T.xtq[:], T.xtqs[:], T.xt[:], c)
+        mm(bank[:, 0:128], "wlq", 0, 128, "xtq", 0, 128, True, False, c)
+        return mm(bank[:, 0:128], "wlq", 0, 128, "xtq", 12, 140, False, True)
+
+    ms = scores("zq", "b1q", ("zin", 2 * landing), zo[0], zo[1], c_b1)
+    for b in range(4):
+        mm(T["pd%d" % b][:, 0:192], "epq", 128 * b, 128 * b + 128, "zq", 0, 192, True, False, c_e)
+    cs, c1 = words(ms, T.rm1, T.jk1, 0, T.pt1)
+    m = tolist(T.pt1, T.offl, T.psa, c1)
+    c_l = ts(T.l1[:], T.psa[:, 0:12], T.hcol[:], None, A.add, None, m)
+    vv, vs = pick("vbq", 0, 192, "b1q", 512, T.l1[:, 0:12], c_l)
+    fan([T.vbq[:, 48 * a:48 * a + 48].bitcast(dt.uint8) for a in range(3)], [T.lvq[:, 48 * (2 - a):48 * (2 - a) + 48].bitcast(dt.uint8) for a in range(3)], "vin", vv)
+    fan([T.vbqs[:, 48 * a:48 * a + 48] for a in range(3)], [T.lvqs[:, 48 * (2 - a):48 * (2 - a) + 48] for a in range(3)], "vin", vs)
+    need("y", vv, vs)
+    dma("y", T.lvq[:, 144:192].bitcast(dt.uint8), T.vbq[:, 144:192].bitcast(dt.uint8), "dv")
+    dma("y", T.lvqs[:, 144:192], T.vbqs[:, 144:192], "dv")
+    cr = []
+    for b in range(4):
+        m = mm(T["pd%d" % b][:, 0:192], "enq", 128 * b, 128 * b + 128, "vbq", 0, 192, False, True, vv, vs, c_n)
+        if b % 2 == 0:
+            cr.append(copy(T.rt[:, b:768:4], T["pd%d" % b][:, 0:192], m))
+        else:
+            cr.append(act(T.rt[:, b:768:4], T["pd%d" % b][:, 0:192], F.Copy, m))
+    act(T.nbf[:, 0:4], T.nf[:, 0:4], F.Copy, cs)
+    act(T.nbf[:, 8:12], T.nf[:, 4:8], F.Copy)
+    c_r = quant(T.rq[:], T.rqs[:], T.rt[:], *cr)
+    ms = scores("rq", "b2q", c_r, c_b2)
+    cs, c1 = words(ms, T.rm2, T.jk2, 8, T.pt2)
+    act(T.nbf[:, 4:8], T.nf[:, 8:12], F.Copy, cs)
+    c_nb = act(T.nbf[:, 12:16], T.nf[:, 12:16], F.Copy)
+    fan([T.nbf[:, 8 * (a // 2):8 * (a // 2) + 8] for a in range(3)], [T.ln[:, 32 * (2 - a):32 * (2 - a) + 8] for a in range(3)], "nin", c_nb)
+    c_ln3 = act(T.ln[:, 96:104], T.nbf[:, 8:16], F.Copy, c_nb, c_ln)
+    m = tolist(T.pt2, T.offl, T.psa, c1)
+    c_l = ts(T.l2[:, 0:9], T.psa[:, 0:9], T.hcol[:], None, A.add, None, m)
+    wv, ws = pick("v2q", 0, 144, "b2q", 512, T.l2[:, 0:9], c_l)
+    fan([T.v2q[:, 48 * a:48 * a + 48].bitcast(dt.uint8) for a in range(3)], [T.lwq[:, 48 * (2 - a):48 * (2 - a) + 48].bitcast(dt.uint8) for a in range(3)], "win", wv)
+    fan([T.v2qs[:, 48 * a:48 * a + 48] for a in range(3)], [T.lwqs[:, 48 * (2 - a):48 * (2 - a) + 48] for a in range(3)], "win", ws)
+    c_l = ts(T.l2b[:, 0:3], T.psa[:, 9:12], T.hcol[:], None, A.add, None)
+    wo = pick("lwq", 144, 192, "b2q", 512, T.l2b[:, 0:3], c_l)
+
+    c_q = quant(T.wq[:], T.wqs[:], T.wb[:], ("dw", 16))
+    c = ts(T.vi[:], T.r2[:], -1024.0, None, A.add, None)
+    ts(T.ai[:], T.vi[:], 8, None, A.arith_shift_right, None, c)
+    c = ts(T.bi[:], T.vi[:], 255, None, A.bitwise_and, None)
+    c_wt = fill(T.wt[:], -1.0)
+    c1 = ts(T.q1[:], T.ai[:], 48.0, -192.0, A.mult, A.add, c)
+    ts(T.tf[:], T.bi[:], 48.0, None, A.is_lt, None)
+    c = tt(T.q2[:], T.q1[:], T.bi[:], A.add, c1)
+    c_oj = ts(T.ofj[:], T.ofi[:], 28, None, A.bitwise_and, None, c_oi)
+    c = tt(T.pf[:], T.q2[:], T.tf[:], A.mult, c)
+    copy(T.offp[:], T.ofj[:], c_oj)
+    c = ts(T.pt0[:, 0:8:4], T.pf[:], RND, RND, A.add, A.subtract, c)
+    c = tt(T.pt0[:, 8:16:4], T.pf[:], T.pt0[:, 0:8:4], A.subtract, c)
+    m = tolist(T.pt0, T.offp, T.psb, c)
+    c_l = ts(T.pl[:], T.psb[:, 0:12], 192.0, None, A.add, None, m)
+    ov, os_ = pick("o1q", 0, 192, "lvq", 208, T.pl[:, 0:12], c_l, ("vin", 2 * landing), ("dv", 32), ("dz", 64))
+    need("y", ov, os_)
+    dma("y", T.oc[:, 0:768], T.o1q[:].bitcast(dt.uint8), "st")
+    for k in range(4):
+        dma("y", T.osc[4 * k:4 * k + 4, 0:192], T.o1qs[32 * k:32 * k + 4, :], "st")
+    mm(T.psc[:, 0:192], "wq", 0, 128, "o1q", 0, 192, True, False, ov, os_, c_q)
+    need("v", c_ln3, ("nin", landing))
+    c = done("v", V.transpose(T.tr[:], T.ln[:]))
+    for a, q, i, n, o in ((0, 1, 0, 32, 0), (0, 2, 0, 16, 32), (1, 1, 16, 16, 0), (1, 2, 0, 32, 16), (2, 0, 0, 32, 0), (2, 1, 0, 16, 32), (3, 2, 16, 16, 0), (3, 3, 0, 32, 16)):
+        c_t = act(T.wt[0:32, 48 * a + o:48 * a + o + n], T.tr[32 * q:32 * q + 32, 32 * a + i:32 * a + i + n], F.Copy, c, c_wt)
+    need("v", c_t)
+    c = done("v", V.tensor_copy(T.wno[:], T.wt[:, 0:208].indirect(T.pl[:, 0:12])))
+    need("y", c)
+    dma("y", T.wn[:], T.wno[0:8, :], "st")
+    ov, os_ = pick("o2q", 0, 192, "lwq", 208, T.pl[:, 0:12], ("win", 2 * landing), wo[0], wo[1])
+    need("y", ov)
+    dma("y", T.oc[:, 768:1536], T.o2q[:].bitcast(dt.uint8), "st")
+    need("s", os_)
+    for k in range(4):
+        dma("s", T.osc[4 * k:4 * k + 4, 192:384], T.o2qs[32 * k:32 * k + 4, :], "st")
+    m = mm(T.psc[:, 0:192], "wq", 0, 128, "o2q", 0, 192, False, True, ov, os_)
+    c = copy(T.ysb[:], T.psc[:, 0:192], m)
+    need("y", c)
+    dma("y", T.y[:], T.ysb[:], "st")
+
+    need("y", *[(qsem[q], cnt[q]) for q in cnt])
+    need("y", ("st", 16 * stores[0]))
+    need("g", ("left", left[0]))

@@ -3,7 +3,7 @@ from concourse.mybir import dt, AluOpType, AxisListType, ActivationFunctionType
 
 A = AluOpType
 F = ActivationFunctionType
-TOK, CAP, NR = 192, 48, 4
+NR = 4
 LOW = -1e29
 RND = 1.5 * 2.0 ** 27
 
@@ -26,21 +26,21 @@ for _n, _w in (("xq", 192), ("cq", 128), ("wq", 128), ("b1q", 512), ("b2q", 512)
                ("rq", 192), ("o1q", 192), ("o2q", 192)):
     SCRATCH[_n] = _codes(_w)
     SCRATCH[_n + "s"] = _plane(_w)
-for _n, _w in (("xb", 768), ("cb", 512), ("wb", 512), ("bm1", 2048), ("bm2", 2048), ("trb", 1024), ("wlb", 512), ("epb", 520), ("enb", 520),
-               ("ot", 512), ("ab", 560), ("xt", 560), ("rt", 768), ("zz", 512), ("on1", 520), ("t1", 128), ("im", 128), ("zr", 256),
+for _n, _w in (("xb", 768), ("cb", 512), ("wb", 512), ("bm1", 2048), ("bm2", 2048), ("trb", 516), ("wlb", 512), ("epb", 516), ("enb", 516),
+               ("ot", 512), ("ab", 560), ("xt", 560), ("rt", 768), ("zz", 516), ("on1", 128), ("t1", 128), ("im", 128), ("zr", 256),
                ("jk1", 1024), ("jk2", 1024), ("nbf", 16), ("ln", 128), ("tr", 128)):
     SCRATCH[_n] = _sb(_w, "bfloat16")
 for _n, _w in (("rma", 16), ("ua", 16), ("r2", 2), ("hc", 2), ("nl", 2), ("tk", 4), ("ib", 12), ("ibc", 12), ("vl", 1), ("hcol", 1),
-               ("df", 1), ("e0", 1), ("e4", 1), ("off", 6), ("rm1", 1024), ("rm2", 1024), ("nf", 16), ("pt0", 24), ("pt1", 24), ("pt2", 24),
+               ("df", 1), ("e0", 1), ("e4", 1), ("off", 3), ("rm1", 1024), ("rm2", 1024), ("nf", 16), ("pt0", 24), ("pt1", 24), ("pt2", 24),
                ("tf", 2), ("q1", 2), ("q2", 2), ("pf", 2), ("wt", 208), ("wno", 192), ("ysb", 192)):
     SCRATCH[_n] = _sb(_w, "float32")
-for _n, _w in (("pi", 1), ("pa", 1), ("pb", 1), ("gi", 1), ("ui", 1), ("ti", 1), ("hi", 1), ("ofi", 6), ("ofj", 6), ("vi", 2), ("ai", 2), ("bi", 2)):
+for _n, _w in (("pi", 1), ("pa", 1), ("pb", 1), ("gi", 1), ("ui", 1), ("ti", 1), ("hi", 1), ("vi", 2), ("ai", 2), ("bi", 2)):
     SCRATCH[_n] = _sb(_w, "int32")
-for _n, _w in (("zl", 12), ("zl2", 4), ("pl", 12), ("l1", 12), ("l2", 12), ("l2b", 4), ("offl", 6), ("offp", 6)):
+for _n, _w in (("zl", 12), ("zl2", 4), ("pl", 12), ("l1", 12), ("l2", 12), ("l2b", 4), ("ofo", 4), ("ofa", 12)):
     SCRATCH[_n] = _sb(_w, "uint16")
 for _n in ("psa", "psb", "psc", "psd", "pd0", "pd1", "pd2", "pd3"):
     SCRATCH[_n] = ("psum", [128, 512], "float32")
-SEMAPHORES = ["qv", "qs", "qt", "qg", "dx", "dco", "db1", "db2", "dw", "dz", "dv", "st", "zin", "vin", "win", "nin", "left"]
+SEMAPHORES = ["qv", "qs", "qt", "qg", "dx", "dco", "db1", "db2", "dw", "dz", "dv", "do", "st", "zin", "vin", "win", "nin", "oin", "left"]
 
 
 def _mask(topo, src, peers):
@@ -48,12 +48,11 @@ def _mask(topo, src, peers):
     for c in peers:
         e = topo.engines(src, c)
         if topo.die(src) != topo.die(c):
-            pick = e[far * 8:far * 8 + 8:2]
+            out[c] = e[far * 8:far * 8 + 8:2]
             far += 1
         else:
-            pick = e[1 + near * 8:9 + near * 8:2]
+            out[c] = e[1 + near * 8:9 + near * 8:2]
             near += 1
-        out[c] = pick
     return out
 
 
@@ -142,54 +141,54 @@ def rank_program(g, core, T, topo):
     dma("s", T.cb[:], T.co[:], "dco")
 
     c_pi = done("g", g.iota(T.pi[:], [[0, 1]], 0, 1))
+    c_on = fill(T.on1[:], 1.0)
+    c_zz = fill(T.zz[:], 0.0)
+    c_tr = fill(T.trb[:], 1.0)
+    c_ot = act(T.ot[:], T.zz[:, 0:512], F.Copy, c_zz)
+    need("g", c_on)
+    c_t1 = done("g", g.affine_select(T.t1[:], T.on1[:], [[1, 128]], A.is_gt, 0.0, 0, -1))
+    ts(T.gi[:], T.pi[:], 4, None, A.arith_shift_right, None, c_pi)
+    c = ts(T.ui[:], T.pi[:], 2, 3, A.arith_shift_right, A.bitwise_and)
+    ts(T.ti[:], T.pi[:], 3 if rank < 2 else 0, None, A.bitwise_and, None)
+    c = tt(T.df[:], T.gi[:], T.ui[:], A.subtract, c)
+    c_tr = fill(T.trb[:, 2:516:4], 0.0, c_tr)
+    ts(T.e0[:], T.df[:], 0.0, None, A.is_equal, None, c)
+    c = ts(T.e4[:], T.df[:], 4.0, None, A.is_equal, None)
+    c_rm = fill(T.rma[:], LOW)
+    for k, v in enumerate(((-16.0, -16.0, -12.0), (-8.0, -8.0, -4.0))[rank % 2]):
+        c = ts(T.off[:, k:k + 1], T.ti[:], v, (T.e4 if k else T.e0)[:], A.add, A.mult, c)
+    c_of = ts(T.ofo[:, 0:3], T.off[:], 16.0, None, A.add, None, c)
+    need("g", c_t1, c_tr)
+    c_tri = done("g", g.affine_select(T.trb[:, 1:513:4], T.t1[:], [[1, 128]], A.not_equal, 1024.0, 0, -1))
+    need("g", c_ot)
+    c_ot = done("g", g.iota(T.ot[:, 3:4 * rank + 4:4], [[2, rank + 1]], 2 * (3 - rank), 0, allow_small_or_imprecise_dtypes=True))
+    if rank < NR - 1:
+        c_ot = done("g", g.iota(T.ot[:, 4 * rank + 7:16:4], [[2, NR - 1 - rank]], 0, 0, allow_small_or_imprecise_dtypes=True))
     c_im = done("g", g.iota(T.im[:], [[0, 8], [1, 16]], 0, 0, allow_small_or_imprecise_dtypes=True))
     c_ib = done("g", g.iota(T.ib[:], [[256, 4], [16, 3]], 1024, 0, allow_small_or_imprecise_dtypes=True))
-    c_zz = fill(T.zz[:], 0.0)
-    c_on = fill(T.on1[:], 1.0)
-    c_tr = fill(T.trb[:], 1.0)
-    c_tr = fill(T.trb[:, 1:512:4], 0.0, c_tr)
-    c_ot = fill(T.ot[:], 0.0)
-    c_zr = fill(T.zr[:], 0.0)
-    c_rm = fill(T.rma[:], LOW)
-    c_ln = fill(T.ln[:], 0.0)
-    c_zr = fill(T.zr[:, 128:129], LOW, c_zr)
-    for d in range(NR):
-        rel = (d - rank - 1) % NR
-        if rel:
-            c_ot = fill(T.ot[:, 3 + 4 * d:4 + 4 * d], 2.0 * rel, c_ot)
-    for k, b in enumerate(("bm1", "bm2")):
+    own = slice(3 * rank, 3 * rank + 3)
+    fan([T.ofo[:, 0:3]] * 3, [T.ofa[:, own]] * 3, "oin", c_of)
+    need("y", c_of)
+    dma("y", T.ofa[:, own], T.ofo[:, 0:3], "do")
+
+    def book(k):
+        b = (T.bm1, T.bm2)[k]
         for h in range(4):
-            c_z = act(T[b][:, 512 * h:512 * h + 512], T.zz[:], F.Copy, c_zz)
+            c_z = act(b[:, 512 * h:512 * h + 512], T.zz[:, 0:512], F.Copy, c_zz)
         need("y", c_z)
         for h in range(4):
-            dma("y", T[b][32 * h:32 * h + 32, 512 * h:512 * h + 512], (T.b1, T.b2)[k][32 * h:32 * h + 32, :], ("db1", "db2")[k])
-    dma("y", T.wb[:], T.w[:], "dw")
-    need("g", c_on)
-    c_t1 = done("g", g.affine_select(T.t1[:], T.on1[:, 0:128], [[1, 128]], A.is_gt, 0.0, 0, -1))
-    need("g", c_t1, c_tr)
-    done("g", g.affine_select(T.trb[:, 0:512:4], T.t1[:], [[1, 128]], A.not_equal, 1024.0, 0, -1))
-    c_tri = done("g", g.affine_select(T.trb[:, 513:1024:4], T.t1[:], [[1, 128]], A.not_equal, 1024.0, 0, -1))
-    c_ep = done("g", g.affine_select(T.epb[:], T.on1[:], [[1, 520]], A.is_equal, 0.0, -4, -4))
-    need("s", c_ep)
-    c_en = done("s", SC.activation(T.enb[:], T.epb[:], F.Copy, scale=-1.0))
-    ts(T.pa[:], T.pi[:], 112, None, A.bitwise_and, None, c_pi)
-    ts(T.pb[:], T.pi[:], 15, None, A.bitwise_and, None)
-    c_vl = ts(T.vl[:], T.pi[:], 64.0, None, A.is_ge, None)
-    ts(T.gi[:], T.pi[:], 4, None, A.arith_shift_right, None)
-    ts(T.ui[:], T.pi[:], 2, 3, A.arith_shift_right, A.bitwise_and)
-    ts(T.ti[:], T.pi[:], 3, None, A.bitwise_and, None)
-    c_h = ts(T.hi[:], T.pi[:], 5, None, A.arith_shift_right, None)
-    copy(T.tk[:, 0:1], T.pa[:], c_vl)
-    copy(T.tk[:, 1:2], T.pb[:])
-    ts(T.tk[:, 2:3], T.pa[:], 64.0, T.vl[:], A.add, A.mult)
-    c_tk = ts(T.tk[:, 3:4], T.pb[:], T.vl[:], None, A.mult, None)
-    c_ib = ts(T.ibc[:], T.ib[:], RND, None, A.add, None, c_ib)
-    c_df = tt(T.df[:], T.gi[:], T.ui[:], A.subtract, c_h)
-    c_hc = ts(T.hcol[:], T.hi[:], 128.0, None, A.mult, None)
+            dma("y", b[32 * h:32 * h + 32, 512 * h:512 * h + 512], (T.b1, T.b2)[k][32 * h:32 * h + 32, :], ("db1", "db2")[k])
+    book(0)
+    c_ep0 = act(T.epb[:], T.zz[:], F.Copy)
 
     c_q = quant(T.cq[:], T.cqs[:], T.cb[:], ("dco", 16))
-    quant(T.trq[:], T.trqs[:], T.trb[:], c_tri)
+    for k in range(2):
+        quant(T.trq[:, 128 * k:128 * k + 128], T.trqs[:, 128 * k:128 * k + 128], T.trb[:, 1 - k:513 - k], c_tri)
     c_x = quant(T.xq[:], T.xqs[:], T.xb[:], ("dx", 16))
+    ts(T.pa[:], T.pi[:], 112, None, A.bitwise_and, None)
+    ts(T.pb[:], T.pi[:], 15, None, A.bitwise_and, None)
+    c_vl = ts(T.vl[:], T.pi[:], 64.0, None, A.is_ge, None)
+    c_ln = fill(T.ln[:], 0.0)
     need("y", c_q)
     for b in ("lvq", "lwq"):
         dma("y", T[b][:, 192:208].bitcast(dt.uint8), T.cq[:, 64:80].bitcast(dt.uint8), "dz")
@@ -203,10 +202,15 @@ def rank_program(g, core, T, topo):
     s0 = scan(T.rma[:, 1:5], T.zz[:, 0:4], T.psa[:, 0:4], m0, c_rm)
     s1 = scan(T.rma[:, 9:13], T.zz[:, 0:4], T.psb[:, 0:4], m1)
     u0 = ts(T.ua[:, 0:5], T.rma[:, 0:5], T.rma[:, 4:5], None, A.is_equal, None, s0)
-    u1 = ts(T.ua[:, 8:13], T.rma[:, 8:13], T.rma[:, 12:13], T.vl[:], A.is_equal, A.mult, s1)
-    tt(T.ot[:, 0:16:4], T.ua[:, 1:5], T.ua[:, 0:4], A.subtract, u0)
+    u1 = ts(T.ua[:, 8:13], T.rma[:, 8:13], T.rma[:, 12:13], T.vl[:], A.is_equal, A.mult, s1, c_vl)
+    tt(T.ot[:, 0:16:4], T.ua[:, 1:5], T.ua[:, 0:4], A.subtract, u0, c_ot)
     o1 = tt(T.ot[:, 1:16:4], T.ua[:, 9:13], T.ua[:, 8:12], A.subtract, u1)
     c_o = quant(T.otq[:], T.otqs[:], T.ot[:], o1)
+    copy(T.tk[:, 0:1], T.pa[:])
+    copy(T.tk[:, 1:2], T.pb[:])
+    ts(T.tk[:, 2:3], T.pa[:], 64.0, T.vl[:], A.add, A.mult)
+    c_tk = ts(T.tk[:, 3:4], T.pb[:], T.vl[:], None, A.mult, None)
+    c_ib = ts(T.ibc[:], T.ib[:], RND, None, A.add, None, c_ib)
     m0 = mm(T.psc[:, 0:128], "trq", 0, 128, "otq", 0, 128, True, True, c_o)
     m1 = mm(T.psd[:, 0:128], "trq", 128, 256, "otq", 0, 128, True, True)
     need("v", m0)
@@ -218,7 +222,7 @@ def rank_program(g, core, T, topo):
     for s in range(2):
         c_nl.append(ts(T.nl[:, s:s + 1], T.hc[:, s:s + 1], RND, T.r2[:, s:s + 1], A.subtract, A.subtract, c_hcv))
     for t in range(4):
-        ts(T.ab[:, 512 + t:560:4], T.ibc[:], T.hc[:, t // 2:t // 2 + 1], T.tk[:, t:t + 1], A.is_equal, A.mult)
+        ts(T.ab[:, 512 + t:560:4], T.ibc[:], T.hc[:, t // 2:t // 2 + 1], T.tk[:, t:t + 1], A.is_equal, A.mult, c_tk, c_ib)
     for t in range(4):
         c_a = ts(T.ab[:, t:512:4], T.im[:], T.nl[:, t // 2:t // 2 + 1], 0.0, A.add, A.is_equal, c_nl[t // 2], c_im)
     c_a = quant(T.abq[:], T.abqs[:], T.ab[:], c_a)
@@ -230,56 +234,66 @@ def rank_program(g, core, T, topo):
     c_l = copy(T.zl2[:, 0:3], T.psa[:, 125:128])
     zo = pick("zq", 144, 192, "xq", 192, T.zl2[:, 0:3], c_l)
 
+    need("g", c_ep0)
+    c_ep = done("g", g.affine_select(T.epb[:, 4:516:4], T.on1[:], [[1, 128]], A.is_equal, 0.0, 0, -1))
+    need("s", c_ep)
+    c_en = done("s", SC.activation(T.enb[:], T.epb[:], F.Copy, scale=-1.0))
+    book(1)
+    dma("y", T.wb[:], T.w[:], "dw")
     c_b1 = quant(T.b1q[:], T.b1qs[:], T.bm1[:], ("db1", 64))
-    for b in range(4):
-        c_e = quant(T.epq[:, 128 * b:128 * b + 128], T.epqs[:, 128 * b:128 * b + 128], T.epb[:, 4 - b:516 - b], c_ep)
+    c_zr = fill(T.zr[:], 0.0)
     c_w = fill(T.wlb[:], 0.0)
-    c_e0 = ts(T.e0[:], T.df[:], 0.0, None, A.is_equal, None)
-    c_e4 = ts(T.e4[:], T.df[:], 4.0, None, A.is_equal, None)
+    c_hi = ts(T.hi[:], T.pi[:], 5, None, A.arith_shift_right, None)
+    c_zr = fill(T.zr[:, 128:129], LOW, c_zr)
     for t in range(4):
         c_w = ts(T.wlb[:, 129 * t:128 * t + 128:4], T.im[:, 0:32], T.tk[:, 1:2], None, A.is_equal, None, c_w)
-    for k, (c, e) in enumerate(((-16., T.e0), (-16., T.e4), (-12., T.e4), (-8., T.e0), (-8., T.e4), (-4., T.e4))):
-        c_f = ts(T.off[:, k:k + 1], T.ti[:], c, e[:], A.add, A.mult, c_e4)
-    c_w = quant(T.wlq[:], T.wlqs[:], T.wlb[:], c_w)
-    c_ol = ts(T.offl[:], T.off[:], 16.0, None, A.add, None, c_f)
-    c_oi = ts(T.ofi[:], T.off[:], 16.0, None, A.add, None)
-    for b in range(4):
-        c_n = quant(T.enq[:, 128 * b:128 * b + 128], T.enqs[:, 128 * b:128 * b + 128], T.enb[:, 4 - b:516 - b], c_en)
-    fill(T.xt[:, 96:560], 0.0)
+    c_hc = ts(T.hcol[:], T.hi[:], 128.0, None, A.mult, None, c_hi)
     for p in (T.pt0, T.pt1, T.pt2):
         fill(p[:], 0.0)
-    c_b2 = quant(T.b2q[:], T.b2qs[:], T.bm2[:], ("db2", 64))
+    fill(T.xt[:, 96:560], 0.0)
+    c_w = quant(T.wlq[:], T.wlqs[:], T.wlb[:], c_w)
+    for b in range(4):
+        c_e = quant(T.epq[:, 128 * b:128 * b + 128], T.epqs[:, 128 * b:128 * b + 128], T.epb[:, 4 - b:516 - b], c_ep)
+    for b in range(4):
+        c_n = quant(T.enq[:, 128 * b:128 * b + 128], T.enqs[:, 128 * b:128 * b + 128], T.enb[:, 4 - b:516 - b], c_en)
 
-    banks = ("psa", "psb", "psc", "psd")
+    parts = (("psa", 0, 0, 1), ("psb", 0, 1, 1), ("psc", 0, 2, 2), ("psd", 1, 0, 2), ("pd2", 1, 2, 1), ("pd3", 1, 3, 1))
 
-    def scores(tok, book, *deps):
-        return [mm(T[banks[k]][:, 0:256], tok, 64 * (k // 2), 64 * (k // 2) + 128, book, 256 * (k % 2), 256 * (k % 2) + 256, True, True, *deps)
-                for k in range(4)]
+    def scores(tok, bk, *deps):
+        return [mm(T[b][:, 0:128 * n], tok, 64 * s, 64 * s + 128, bk, 128 * h, 128 * (h + n), True, True, *deps) for b, s, h, n in parts]
 
     def words(ms, rm, jk, base, pt):
-        for k in range(4):
-            c = scan(rm[:, 256 * k:256 * k + 256], T.zr[:], T[banks[k]][:, 0:256], ms[k])
-            for h in range(2):
-                a = 256 * k + 128 * h
+        for k, (b, s, h, n) in enumerate(parts):
+            e = 512 * s + 128 * h
+            c = scan(rm[:, e:e + 128 * n], T.zr[:, 0:128 * n], T[b][:, 0:128 * n], ms[k])
+            if k == len(parts) - 1:
+                break
+            for a in range(e, e + 128 * n, 128):
                 need("s", c)
                 cs = done("s", SC.activation(jk[:, a:a + 128], rm[:, a:a + 128], F.Sign, bias=rm[:, a + 127:a + 128], scale=-1.0,
-                                             accum_out=T.nf[:, base + 2 * k + h:base + 2 * k + h + 1]))
-        c1 = ts(pt[:, 0:8], T.nf[:, base:base + 8], RND, RND, A.add, A.subtract, cs)
+                                             accum_out=T.nf[:, base + a // 128:base + a // 128 + 1]))
+        c1 = ts(jk[:, e:e + 128], rm[:, e:e + 128], rm[:, e + 127:e + 128], None, A.is_lt, None, c)
+        need("v", c1)
+        cv = done("v", V.tensor_reduce(T.nf[:, base + 7:base + 8], jk[:, e:e + 128], AxisListType.X, A.add))
+        c1 = ts(pt[:, 0:8], T.nf[:, base:base + 8], RND, RND, A.add, A.subtract, cs, cv)
         c1 = tt(pt[:, 8:16], T.nf[:, base:base + 8], pt[:, 0:8], A.subtract, c1)
-        return cs, c1
+        return cs, cv, c, c1
 
     def tolist(pt, off, bank, c1):
         need("v", c1)
-        c = done("v", V.tensor_copy(T.xt[:, 0:96], pt[:, 0:24].indirect(off[:, 0:6])))
+        c = done("v", V.tensor_copy(T.xt[:, 0:96], pt[:, 0:24].indirect(off)))
         c = quant(T.xtq[:], T.xtqs[:], T.xt[:], c)
         mm(bank[:, 0:128], "wlq", 0, 128, "xtq", 0, 128, True, False, c)
         return mm(bank[:, 0:128], "wlq", 0, 128, "xtq", 12, 140, False, True)
 
     ms = scores("zq", "b1q", ("zin", 2 * landing), zo[0], zo[1], c_b1)
-    for b in range(4):
+    for b in range(2):
         mm(T["pd%d" % b][:, 0:192], "epq", 128 * b, 128 * b + 128, "zq", 0, 192, True, False, c_e)
-    cs, c1 = words(ms, T.rm1, T.jk1, 0, T.pt1)
-    m = tolist(T.pt1, T.offl, T.psa, c1)
+    cs, cv, c_sc, c1 = words(ms, T.rm1, T.jk1, 0, T.pt1)
+    for b in range(2, 4):
+        mm(T["pd%d" % b][:, 0:192], "epq", 128 * b, 128 * b + 128, "zq", 0, 192, True, False, c_sc)
+    need("v", ("oin", landing), ("do", 16))
+    m = tolist(T.pt1, T.ofa[:, 0:6], T.psa, c1)
     c_l = ts(T.l1[:], T.psa[:, 0:12], T.hcol[:], None, A.add, None, m)
     vv, vs = pick("vbq", 0, 192, "b1q", 512, T.l1[:, 0:12], c_l)
     fan([T.vbq[:, 48 * a:48 * a + 48].bitcast(dt.uint8) for a in range(3)], [T.lvq[:, 48 * (2 - a):48 * (2 - a) + 48].bitcast(dt.uint8) for a in range(3)], "vin", vv)
@@ -287,6 +301,7 @@ def rank_program(g, core, T, topo):
     need("y", vv, vs)
     dma("y", T.lvq[:, 144:192].bitcast(dt.uint8), T.vbq[:, 144:192].bitcast(dt.uint8), "dv")
     dma("y", T.lvqs[:, 144:192], T.vbqs[:, 144:192], "dv")
+    c_b2 = quant(T.b2q[:], T.b2qs[:], T.bm2[:], ("db2", 64))
     cr = []
     for b in range(4):
         m = mm(T["pd%d" % b][:, 0:192], "enq", 128 * b, 128 * b + 128, "vbq", 0, 192, False, True, vv, vs, c_n)
@@ -294,16 +309,16 @@ def rank_program(g, core, T, topo):
             cr.append(copy(T.rt[:, b:768:4], T["pd%d" % b][:, 0:192], m))
         else:
             cr.append(act(T.rt[:, b:768:4], T["pd%d" % b][:, 0:192], F.Copy, m))
-    act(T.nbf[:, 0:4], T.nf[:, 0:4], F.Copy, cs)
+    act(T.nbf[:, 0:4], T.nf[:, 0:4], F.Copy, cs, cv)
     act(T.nbf[:, 8:12], T.nf[:, 4:8], F.Copy)
     c_r = quant(T.rq[:], T.rqs[:], T.rt[:], *cr)
     ms = scores("rq", "b2q", c_r, c_b2)
-    cs, c1 = words(ms, T.rm2, T.jk2, 8, T.pt2)
-    act(T.nbf[:, 4:8], T.nf[:, 8:12], F.Copy, cs)
+    cs, cv, c_sc, c1 = words(ms, T.rm2, T.jk2, 8, T.pt2)
+    act(T.nbf[:, 4:8], T.nf[:, 8:12], F.Copy, cs, cv)
     c_nb = act(T.nbf[:, 12:16], T.nf[:, 12:16], F.Copy)
     fan([T.nbf[:, 8 * (a // 2):8 * (a // 2) + 8] for a in range(3)], [T.ln[:, 32 * (2 - a):32 * (2 - a) + 8] for a in range(3)], "nin", c_nb)
     c_ln3 = act(T.ln[:, 96:104], T.nbf[:, 8:16], F.Copy, c_nb, c_ln)
-    m = tolist(T.pt2, T.offl, T.psa, c1)
+    m = tolist(T.pt2, T.ofa[:, 0:6], T.psa, c1)
     c_l = ts(T.l2[:, 0:9], T.psa[:, 0:9], T.hcol[:], None, A.add, None, m)
     wv, ws = pick("v2q", 0, 144, "b2q", 512, T.l2[:, 0:9], c_l)
     fan([T.v2q[:, 48 * a:48 * a + 48].bitcast(dt.uint8) for a in range(3)], [T.lwq[:, 48 * (2 - a):48 * (2 - a) + 48].bitcast(dt.uint8) for a in range(3)], "win", wv)
@@ -319,12 +334,10 @@ def rank_program(g, core, T, topo):
     c1 = ts(T.q1[:], T.ai[:], 48.0, -192.0, A.mult, A.add, c)
     ts(T.tf[:], T.bi[:], 48.0, None, A.is_lt, None)
     c = tt(T.q2[:], T.q1[:], T.bi[:], A.add, c1)
-    c_oj = ts(T.ofj[:], T.ofi[:], 28, None, A.bitwise_and, None, c_oi)
     c = tt(T.pf[:], T.q2[:], T.tf[:], A.mult, c)
-    copy(T.offp[:], T.ofj[:], c_oj)
     c = ts(T.pt0[:, 0:8:4], T.pf[:], RND, RND, A.add, A.subtract, c)
     c = tt(T.pt0[:, 8:16:4], T.pf[:], T.pt0[:, 0:8:4], A.subtract, c)
-    m = tolist(T.pt0, T.offp, T.psb, c)
+    m = tolist(T.pt0, T.ofa[:, 6:12], T.psb, c)
     c_l = ts(T.pl[:], T.psb[:, 0:12], 192.0, None, A.add, None, m)
     ov, os_ = pick("o1q", 0, 192, "lvq", 208, T.pl[:, 0:12], c_l, ("vin", 2 * landing), ("dv", 32), ("dz", 64))
     need("y", ov, os_)

@@ -21,18 +21,18 @@ def _sb(n, d):
 
 
 SCRATCH = {}
-for _n, _w in (("xq", 192), ("cq", 128), ("wq", 128), ("b1q", 512), ("b2q", 512), ("trq", 256), ("wlq", 128), ("epq", 512), ("enq", 512),
-               ("otq", 128), ("abq", 140), ("xtq", 140), ("zsq", 144), ("zq", 192), ("vbq", 192), ("lvq", 208), ("v2q", 144), ("lwq", 208),
-               ("rq", 192), ("o1q", 192), ("o2q", 192)):
+for _n, _w in (("xq", 192), ("cq", 128), ("wq", 128), ("p1q", 128), ("b1q", 512), ("b2q", 512), ("trq", 256), ("wlq", 128), ("epq", 512),
+               ("otq", 128), ("abq", 140), ("xtq", 140), ("xpq", 140), ("zsq", 144), ("zq", 192), ("vbq", 192), ("lvq", 208), ("v2q", 144),
+               ("lwq", 208), ("rq", 192), ("o1q", 192), ("o2q", 192)):
     SCRATCH[_n] = _codes(_w)
     SCRATCH[_n + "s"] = _plane(_w)
-for _n, _w in (("xb", 768), ("cb", 512), ("wb", 512), ("bm1", 2048), ("bm2", 2048), ("trb", 516), ("wlb", 512), ("epb", 516), ("enb", 516),
-               ("ot", 512), ("ab", 560), ("xt", 560), ("rt", 768), ("zz", 516), ("on1", 128), ("t1", 128), ("im", 128), ("zr", 256),
+for _n, _w in (("xb", 768), ("cb", 512), ("wb", 512), ("pb1", 512), ("bm1", 2048), ("bm2", 2048), ("trb", 516), ("wlb", 512), ("epb", 516),
+               ("ot", 512), ("ab", 560), ("xt", 560), ("xp", 560), ("rt", 768), ("zz", 516), ("on1", 128), ("t1", 128), ("im", 128), ("zr", 256),
                ("jk1", 1024), ("jk2", 1024), ("nbf", 16), ("ln", 128), ("tr", 128)):
     SCRATCH[_n] = _sb(_w, "bfloat16")
 for _n, _w in (("rma", 16), ("ua", 16), ("r2", 2), ("hc", 2), ("nl", 2), ("tk", 4), ("ib", 12), ("ibc", 12), ("vl", 1), ("hcol", 1),
                ("df", 1), ("e0", 1), ("e4", 1), ("off", 3), ("rm1", 1024), ("rm2", 1024), ("nf", 16), ("pt0", 24), ("pt1", 24), ("pt2", 24),
-               ("tf", 2), ("q1", 2), ("q2", 2), ("pf", 2), ("wt", 208), ("wno", 192), ("ysb", 192)):
+               ("tf", 2), ("q1", 2), ("q2", 2), ("pf", 2), ("wt", 208), ("wno", 192), ("ysb", 192), ("db", 512), ("dq", 576), ("g3", 192)):
     SCRATCH[_n] = _sb(_w, "float32")
 for _n, _w in (("pi", 1), ("pa", 1), ("pb", 1), ("gi", 1), ("ui", 1), ("ti", 1), ("hi", 1), ("vi", 2), ("ai", 2), ("bi", 2)):
     SCRATCH[_n] = _sb(_w, "int32")
@@ -40,7 +40,7 @@ for _n, _w in (("zl", 12), ("zl2", 4), ("pl", 12), ("l1", 12), ("l2", 12), ("l2b
     SCRATCH[_n] = _sb(_w, "uint16")
 for _n in ("psa", "psb", "psc", "psd", "pd0", "pd1", "pd2", "pd3"):
     SCRATCH[_n] = ("psum", [128, 512], "float32")
-SEMAPHORES = ["qv", "qs", "qt", "qg", "dx", "dco", "db1", "db2", "dw", "dz", "dv", "do", "st", "zin", "vin", "win", "nin", "oin", "left"]
+SEMAPHORES = ["qv", "qs", "qt", "qg", "dx", "dco", "dp1", "db1", "db2", "dw", "dz", "dv", "do", "st", "zin", "vin", "win", "nin", "oin", "left"]
 
 
 def _mask(topo, src, peers):
@@ -137,14 +137,22 @@ def rank_program(g, core, T, topo):
             left[0] += len(emask[c])
         g.remote_dma_fused(tr, local_sem=S["left"])
 
+    def fan_codes(src, dst, sem, c):
+        fan([T[src][:, 48 * a:48 * a + 48].bitcast(dt.uint8) for a in range(3)],
+            [T[dst][:, 48 * (2 - a):48 * (2 - a) + 48].bitcast(dt.uint8) for a in range(3)], sem, c)
+
+    def fan_scales(src, dst, sem, c):
+        fan([T[src + "s"][:, 48 * a:48 * a + 48] for a in range(3)], [T[dst + "s"][:, 48 * (2 - a):48 * (2 - a) + 48] for a in range(3)], sem, c)
+
     dma("y", T.xb[:], T.x[:], "dx")
-    dma("s", T.cb[:], T.co[:], "dco")
+    dma("s", T.cb[:, 0:4 * NR], T.co[:, 0:4 * NR], "dco")
 
     c_pi = done("g", g.iota(T.pi[:], [[0, 1]], 0, 1))
     c_on = fill(T.on1[:], 1.0)
     c_zz = fill(T.zz[:], 0.0)
     c_tr = fill(T.trb[:], 1.0)
     c_ot = act(T.ot[:], T.zz[:, 0:512], F.Copy, c_zz)
+    c_ep0 = act(T.epb[:], T.zz[:], F.Copy)
     need("g", c_on)
     c_t1 = done("g", g.affine_select(T.t1[:], T.on1[:], [[1, 128]], A.is_gt, 0.0, 0, -1))
     ts(T.gi[:], T.pi[:], 4, None, A.arith_shift_right, None, c_pi)
@@ -158,6 +166,7 @@ def rank_program(g, core, T, topo):
     for k, v in enumerate(((-16.0, -16.0, -12.0), (-8.0, -8.0, -4.0))[rank % 2]):
         c = ts(T.off[:, k:k + 1], T.ti[:], v, (T.e4 if k else T.e0)[:], A.add, A.mult, c)
     c_of = ts(T.ofo[:, 0:3], T.off[:], 16.0, None, A.add, None, c)
+    c_cb = fill(T.cb[:, 4 * NR:512], 0.0)
     need("g", c_t1, c_tr)
     c_tri = done("g", g.affine_select(T.trb[:, 1:513:4], T.t1[:], [[1, 128]], A.not_equal, 1024.0, 0, -1))
     need("g", c_ot)
@@ -166,22 +175,24 @@ def rank_program(g, core, T, topo):
         c_ot = done("g", g.iota(T.ot[:, 4 * rank + 7:16:4], [[2, NR - 1 - rank]], 0, 0, allow_small_or_imprecise_dtypes=True))
     c_im = done("g", g.iota(T.im[:], [[0, 8], [1, 16]], 0, 0, allow_small_or_imprecise_dtypes=True))
     c_ib = done("g", g.iota(T.ib[:], [[256, 4], [16, 3]], 1024, 0, allow_small_or_imprecise_dtypes=True))
+    need("g", c_ep0)
+    c_ep = done("g", g.affine_select(T.epb[:, 4:516:4], T.on1[:], [[1, 128]], A.is_equal, 0.0, 0, -1))
     own = slice(3 * rank, 3 * rank + 3)
     fan([T.ofo[:, 0:3]] * 3, [T.ofa[:, own]] * 3, "oin", c_of)
     need("y", c_of)
     dma("y", T.ofa[:, own], T.ofo[:, 0:3], "do")
 
-    def book(k):
-        b = (T.bm1, T.bm2)[k]
+    for k, b in enumerate((T.bm1, T.bm2)):
         for h in range(4):
             c_z = act(b[:, 512 * h:512 * h + 512], T.zz[:, 0:512], F.Copy, c_zz)
         need("y", c_z)
+        if k == 0:
+            dma("y", T.pb1[:], T.b1[:], "dp1")
         for h in range(4):
             dma("y", b[32 * h:32 * h + 32, 512 * h:512 * h + 512], (T.b1, T.b2)[k][32 * h:32 * h + 32, :], ("db1", "db2")[k])
-    book(0)
-    c_ep0 = act(T.epb[:], T.zz[:], F.Copy)
+    dma("y", T.wb[:], T.w[:], "dw")
 
-    c_q = quant(T.cq[:], T.cqs[:], T.cb[:], ("dco", 16))
+    c_q = quant(T.cq[:], T.cqs[:], T.cb[:], ("dco", 16), c_cb)
     for k in range(2):
         quant(T.trq[:, 128 * k:128 * k + 128], T.trqs[:, 128 * k:128 * k + 128], T.trb[:, 1 - k:513 - k], c_tri)
     c_x = quant(T.xq[:], T.xqs[:], T.xb[:], ("dx", 16))
@@ -189,10 +200,6 @@ def rank_program(g, core, T, topo):
     ts(T.pb[:], T.pi[:], 15, None, A.bitwise_and, None)
     c_vl = ts(T.vl[:], T.pi[:], 64.0, None, A.is_ge, None)
     c_ln = fill(T.ln[:], 0.0)
-    need("y", c_q)
-    for b in ("lvq", "lwq"):
-        dma("y", T[b][:, 192:208].bitcast(dt.uint8), T.cq[:, 64:80].bitcast(dt.uint8), "dz")
-        dma("y", T[b + "s"][:, 192:208], T.cqs[:, 64:80], "dz")
     m0 = mm(T.psa[:, 0:128], "xq", 0, 128, "cq", 0, 128, True, True, c_x)
     m1 = mm(T.psb[:, 0:128], "xq", 64, 192, "cq", 0, 128, True, True)
 
@@ -229,17 +236,22 @@ def rank_program(g, core, T, topo):
     m0 = mm(T.psa[:, 0:128], "abq", 0, 128, "abq", 12, 140, True, True, c_a)
     c_l = copy(T.zl[:, 0:9], T.psa[:, 116:125], m0)
     zv, zs = pick("zsq", 0, 144, "xq", 192, T.zl[:, 0:9], c_l)
-    fan([T.zsq[:, 48 * a:48 * a + 48].bitcast(dt.uint8) for a in range(3)], [T.zq[:, 48 * (2 - a):48 * (2 - a) + 48].bitcast(dt.uint8) for a in range(3)], "zin", zv)
-    fan([T.zsqs[:, 48 * a:48 * a + 48] for a in range(3)], [T.zqs[:, 48 * (2 - a):48 * (2 - a) + 48] for a in range(3)], "zin", zs)
+    fan_codes("zsq", "zq", "zin", zv)
+    fan_scales("zsq", "zq", "zin", zs)
     c_l = copy(T.zl2[:, 0:3], T.psa[:, 125:128])
     zo = pick("zq", 144, 192, "xq", 192, T.zl2[:, 0:3], c_l)
+    need("y", c_q)
+    for b in ("lvq", "lwq"):
+        dma("y", T[b][:, 192:208].bitcast(dt.uint8), T.cq[:, 64:80].bitcast(dt.uint8), "dz")
+        dma("y", T[b + "s"][:, 192:208], T.cqs[:, 64:80], "dz")
 
-    need("g", c_ep0)
-    c_ep = done("g", g.affine_select(T.epb[:, 4:516:4], T.on1[:], [[1, 128]], A.is_equal, 0.0, 0, -1))
-    need("s", c_ep)
-    c_en = done("s", SC.activation(T.enb[:], T.epb[:], F.Copy, scale=-1.0))
-    book(1)
-    dma("y", T.wb[:], T.w[:], "dw")
+    for b in range(4):
+        c_e = quant(T.epq[:, 128 * b:128 * b + 128], T.epqs[:, 128 * b:128 * b + 128], T.epb[:, 4 - b:516 - b], c_ep)
+    c_p1 = quant(T.p1q[:], T.p1qs[:], T.pb1[:], ("dp1", 16))
+    for b in range(4):
+        m = mm(T["pd%d" % b][:, 0:128], "epq", 128 * b, 128 * b + 128, "p1q", 0, 128, True, True, c_p1)
+        need("s", m)
+        c_db = done("s", SC.activation(T.db[:, 128 * b:128 * b + 128], T["pd%d" % b][:, 0:128], F.Copy, scale=-1.0))
     c_b1 = quant(T.b1q[:], T.b1qs[:], T.bm1[:], ("db1", 64))
     c_zr = fill(T.zr[:], 0.0)
     c_w = fill(T.wlb[:], 0.0)
@@ -249,13 +261,20 @@ def rank_program(g, core, T, topo):
         c_w = ts(T.wlb[:, 129 * t:128 * t + 128:4], T.im[:, 0:32], T.tk[:, 1:2], None, A.is_equal, None, c_w)
     c_hc = ts(T.hcol[:], T.hi[:], 128.0, None, A.mult, None, c_hi)
     for p in (T.pt0, T.pt1, T.pt2):
-        fill(p[:], 0.0)
-    fill(T.xt[:, 96:560], 0.0)
+        c_f = fill(p[:], 0.0)
+    for p in (T.xt, T.xp):
+        fill(p[:, 96:560], 0.0)
     c_w = quant(T.wlq[:], T.wlqs[:], T.wlb[:], c_w)
-    for b in range(4):
-        c_e = quant(T.epq[:, 128 * b:128 * b + 128], T.epqs[:, 128 * b:128 * b + 128], T.epb[:, 4 - b:516 - b], c_ep)
-    for b in range(4):
-        c_n = quant(T.enq[:, 128 * b:128 * b + 128], T.enqs[:, 128 * b:128 * b + 128], T.enb[:, 4 - b:516 - b], c_en)
+    c = ts(T.vi[:], T.r2[:], -1024.0, None, A.add, None)
+    ts(T.ai[:], T.vi[:], 8, None, A.arith_shift_right, None, c)
+    c = ts(T.bi[:], T.vi[:], 255, None, A.bitwise_and, None)
+    c_wt = fill(T.wt[:], -1.0)
+    c1 = ts(T.q1[:], T.ai[:], 48.0, -192.0, A.mult, A.add, c)
+    ts(T.tf[:], T.bi[:], 48.0, None, A.is_lt, None)
+    c = tt(T.q2[:], T.q1[:], T.bi[:], A.add, c1)
+    c = tt(T.pf[:], T.q2[:], T.tf[:], A.mult, c)
+    c = ts(T.pt0[:, 0:8:4], T.pf[:], RND, RND, A.add, A.subtract, c, c_f)
+    c_p0 = tt(T.pt0[:, 8:16:4], T.pf[:], T.pt0[:, 0:8:4], A.subtract, c)
 
     parts = (("psa", 0, 0, 1), ("psb", 0, 1, 1), ("psc", 0, 2, 2), ("psd", 1, 0, 2), ("pd2", 1, 2, 1), ("pd3", 1, 3, 1))
 
@@ -279,66 +298,57 @@ def rank_program(g, core, T, topo):
         c1 = tt(pt[:, 8:16], T.nf[:, base:base + 8], pt[:, 0:8], A.subtract, c1)
         return cs, cv, c, c1
 
-    def tolist(pt, off, bank, c1):
+    def spread(pt, off, xt, c1):
         need("v", c1)
-        c = done("v", V.tensor_copy(T.xt[:, 0:96], pt[:, 0:24].indirect(off)))
-        c = quant(T.xtq[:], T.xtqs[:], T.xt[:], c)
-        mm(bank[:, 0:128], "wlq", 0, 128, "xtq", 0, 128, True, False, c)
-        return mm(bank[:, 0:128], "wlq", 0, 128, "xtq", 12, 140, False, True)
+        c = done("v", V.tensor_copy(T[xt][:, 0:96], pt[:, 0:24].indirect(off)))
+        return quant(T[xt + "q"][:], T[xt + "qs"][:], T[xt][:], c)
 
-    ms = scores("zq", "b1q", ("zin", 2 * landing), zo[0], zo[1], c_b1)
-    for b in range(2):
-        mm(T["pd%d" % b][:, 0:192], "epq", 128 * b, 128 * b + 128, "zq", 0, 192, True, False, c_e)
+    def tolist(bank, xt, *deps):
+        mm(bank[:, 0:128], "wlq", 0, 128, xt + "q", 0, 128, True, False, *deps)
+        return mm(bank[:, 0:128], "wlq", 0, 128, xt + "q", 12, 140, False, True)
+
+    ms = scores("zq", "b1q", ("zin", 2 * landing), zo[0], zo[1], c_b1, c_db)
+    md = [mm(T["pd%d" % b][:, 0:192], "epq", 128 * b, 128 * b + 128, "zq", 0, 192, True, True) for b in range(2)]
     cs, cv, c_sc, c1 = words(ms, T.rm1, T.jk1, 0, T.pt1)
-    for b in range(2, 4):
-        mm(T["pd%d" % b][:, 0:192], "epq", 128 * b, 128 * b + 128, "zq", 0, 192, True, False, c_sc)
+    md += [mm(T["pd%d" % b][:, 0:192], "epq", 128 * b, 128 * b + 128, "zq", 0, 192, True, True, c_sc) for b in range(2, 4)]
+    for b in range(3):
+        c_d = act(T.dq[:, 192 * b:192 * b + 192], T["pd%d" % b][:, 0:192], F.Copy, md[b])
     need("v", ("oin", landing), ("do", 16))
-    m = tolist(T.pt1, T.ofa[:, 0:6], T.psa, c1)
-    c_l = ts(T.l1[:], T.psa[:, 0:12], T.hcol[:], None, A.add, None, m)
-    vv, vs = pick("vbq", 0, 192, "b1q", 512, T.l1[:, 0:12], c_l)
-    fan([T.vbq[:, 48 * a:48 * a + 48].bitcast(dt.uint8) for a in range(3)], [T.lvq[:, 48 * (2 - a):48 * (2 - a) + 48].bitcast(dt.uint8) for a in range(3)], "vin", vv)
-    fan([T.vbqs[:, 48 * a:48 * a + 48] for a in range(3)], [T.lvqs[:, 48 * (2 - a):48 * (2 - a) + 48] for a in range(3)], "vin", vs)
+    m = tolist(T.psa, "xt", spread(T.pt1, T.ofa[:, 0:6], "xt", c1))
+    c_b2 = quant(T.b2q[:], T.b2qs[:], T.bm2[:], ("db2", 64))
+    c_l = copy(T.l1[:], T.psa[:, 0:12], m)
+    need("s", c_l)
+    c_g3 = done("s", SC.activation(T.g3[:], T.db[:, 384:512].indirect(T.l1[:, 0:12]), F.Copy))
+    need("v", c_l, c_d, c_db)
+    for b in range(3):
+        done("v", V.tensor_tensor(T.rt[:, b:768:4], T.db[:, 128 * b:128 * b + 128].indirect(T.l1[:, 0:12]), T.dq[:, 192 * b:192 * b + 192], A.add))
+    c = tt(T.rt[:, 3:768:4], T.g3[:], T.pd3[:, 0:192], A.add, c_g3, md[3])
+    c_r = quant(T.rq[:], T.rqs[:], T.rt[:], c)
+    ms = scores("rq", "b2q", c_r, c_b2)
+    vv, vs = pick("vbq", 0, 192, "p1q", 128, T.l1[:, 0:12])
+    fan_scales("vbq", "lvq", "vin", vs)
+    fan_codes("vbq", "lvq", "vin", vv)
     need("y", vv, vs)
     dma("y", T.lvq[:, 144:192].bitcast(dt.uint8), T.vbq[:, 144:192].bitcast(dt.uint8), "dv")
     dma("y", T.lvqs[:, 144:192], T.vbqs[:, 144:192], "dv")
-    c_b2 = quant(T.b2q[:], T.b2qs[:], T.bm2[:], ("db2", 64))
-    cr = []
-    for b in range(4):
-        m = mm(T["pd%d" % b][:, 0:192], "enq", 128 * b, 128 * b + 128, "vbq", 0, 192, False, True, vv, vs, c_n)
-        if b % 2 == 0:
-            cr.append(copy(T.rt[:, b:768:4], T["pd%d" % b][:, 0:192], m))
-        else:
-            cr.append(act(T.rt[:, b:768:4], T["pd%d" % b][:, 0:192], F.Copy, m))
     act(T.nbf[:, 0:4], T.nf[:, 0:4], F.Copy, cs, cv)
     act(T.nbf[:, 8:12], T.nf[:, 4:8], F.Copy)
-    c_r = quant(T.rq[:], T.rqs[:], T.rt[:], *cr)
-    ms = scores("rq", "b2q", c_r, c_b2)
     cs, cv, c_sc, c1 = words(ms, T.rm2, T.jk2, 8, T.pt2)
     act(T.nbf[:, 4:8], T.nf[:, 8:12], F.Copy, cs, cv)
     c_nb = act(T.nbf[:, 12:16], T.nf[:, 12:16], F.Copy)
     fan([T.nbf[:, 8 * (a // 2):8 * (a // 2) + 8] for a in range(3)], [T.ln[:, 32 * (2 - a):32 * (2 - a) + 8] for a in range(3)], "nin", c_nb)
     c_ln3 = act(T.ln[:, 96:104], T.nbf[:, 8:16], F.Copy, c_nb, c_ln)
-    m = tolist(T.pt2, T.ofa[:, 0:6], T.psa, c1)
-    c_l = ts(T.l2[:, 0:9], T.psa[:, 0:9], T.hcol[:], None, A.add, None, m)
+    m = tolist(T.psa, "xt", spread(T.pt2, T.ofa[:, 0:6], "xt", c1))
+    mp = tolist(T.psb, "xp", spread(T.pt0, T.ofa[:, 6:12], "xp", c_p0))
+    c_l = ts(T.l2[:, 0:9], T.psa[:, 0:9], T.hcol[:], None, A.add, None, m, c_hc)
     wv, ws = pick("v2q", 0, 144, "b2q", 512, T.l2[:, 0:9], c_l)
-    fan([T.v2q[:, 48 * a:48 * a + 48].bitcast(dt.uint8) for a in range(3)], [T.lwq[:, 48 * (2 - a):48 * (2 - a) + 48].bitcast(dt.uint8) for a in range(3)], "win", wv)
-    fan([T.v2qs[:, 48 * a:48 * a + 48] for a in range(3)], [T.lwqs[:, 48 * (2 - a):48 * (2 - a) + 48] for a in range(3)], "win", ws)
+    fan_codes("v2q", "lwq", "win", wv)
+    fan_scales("v2q", "lwq", "win", ws)
     c_l = ts(T.l2b[:, 0:3], T.psa[:, 9:12], T.hcol[:], None, A.add, None)
     wo = pick("lwq", 144, 192, "b2q", 512, T.l2b[:, 0:3], c_l)
 
+    c_l = ts(T.pl[:], T.psb[:, 0:12], 192.0, None, A.add, None, mp)
     c_q = quant(T.wq[:], T.wqs[:], T.wb[:], ("dw", 16))
-    c = ts(T.vi[:], T.r2[:], -1024.0, None, A.add, None)
-    ts(T.ai[:], T.vi[:], 8, None, A.arith_shift_right, None, c)
-    c = ts(T.bi[:], T.vi[:], 255, None, A.bitwise_and, None)
-    c_wt = fill(T.wt[:], -1.0)
-    c1 = ts(T.q1[:], T.ai[:], 48.0, -192.0, A.mult, A.add, c)
-    ts(T.tf[:], T.bi[:], 48.0, None, A.is_lt, None)
-    c = tt(T.q2[:], T.q1[:], T.bi[:], A.add, c1)
-    c = tt(T.pf[:], T.q2[:], T.tf[:], A.mult, c)
-    c = ts(T.pt0[:, 0:8:4], T.pf[:], RND, RND, A.add, A.subtract, c)
-    c = tt(T.pt0[:, 8:16:4], T.pf[:], T.pt0[:, 0:8:4], A.subtract, c)
-    m = tolist(T.pt0, T.ofa[:, 6:12], T.psb, c)
-    c_l = ts(T.pl[:], T.psb[:, 0:12], 192.0, None, A.add, None, m)
     ov, os_ = pick("o1q", 0, 192, "lvq", 208, T.pl[:, 0:12], c_l, ("vin", 2 * landing), ("dv", 32), ("dz", 64))
     need("y", ov, os_)
     dma("y", T.oc[:, 0:768], T.o1q[:].bitcast(dt.uint8), "st")
@@ -354,12 +364,12 @@ def rank_program(g, core, T, topo):
     need("y", c)
     dma("y", T.wn[:], T.wno[0:8, :], "st")
     ov, os_ = pick("o2q", 0, 192, "lwq", 208, T.pl[:, 0:12], ("win", 2 * landing), wo[0], wo[1])
+    m = mm(T.psc[:, 0:192], "wq", 0, 128, "o2q", 0, 192, False, True, ov, os_)
     need("y", ov)
     dma("y", T.oc[:, 768:1536], T.o2q[:].bitcast(dt.uint8), "st")
     need("s", os_)
     for k in range(4):
         dma("s", T.osc[4 * k:4 * k + 4, 192:384], T.o2qs[32 * k:32 * k + 4, :], "st")
-    m = mm(T.psc[:, 0:192], "wq", 0, 128, "o2q", 0, 192, False, True, ov, os_)
     c = copy(T.ysb[:], T.psc[:, 0:192], m)
     need("y", c)
     dma("y", T.y[:], T.ysb[:], "st")

@@ -22,21 +22,21 @@ def _sb(n, d):
 
 SCRATCH = {}
 for _n, _w in (("xq", 192), ("cq", 128), ("wq", 128), ("p1q", 128), ("b1q", 512), ("b2q", 512), ("trq", 256), ("wlq", 128), ("epq", 512),
-               ("otq", 128), ("abq", 140), ("xtq", 140), ("xpq", 140), ("zsq", 144), ("zq", 192), ("vbq", 192), ("lvq", 208), ("v2q", 144),
-               ("lwq", 208), ("rq", 192), ("o1q", 192), ("o2q", 192)):
+               ("otq", 128), ("abq", 140), ("xaq", 136), ("xcq", 132), ("xpq", 140), ("zsq", 144), ("zq", 192), ("vbq", 192), ("lvq", 208),
+               ("v2q", 144), ("lwq", 208), ("raq", 128), ("rcq", 128), ("o1q", 192), ("o2q", 192)):
     SCRATCH[_n] = _codes(_w)
     SCRATCH[_n + "s"] = _plane(_w)
 for _n, _w in (("xb", 768), ("cb", 512), ("wb", 512), ("pb1", 512), ("bm1", 2048), ("bm2", 2048), ("trb", 516), ("wlb", 512), ("epb", 516),
-               ("ot", 512), ("ab", 560), ("xt", 560), ("xp", 560), ("rt", 768), ("zz", 516), ("on1", 128), ("t1", 128), ("im", 128), ("zr", 256),
+               ("ot", 512), ("ab", 560), ("xa", 544), ("xc", 528), ("xp", 560), ("rt", 768), ("zz", 516), ("on1", 128), ("t1", 128), ("im", 128),
                ("jk1", 1024), ("jk2", 1024), ("nbf", 16), ("ln", 128), ("tr", 128)):
     SCRATCH[_n] = _sb(_w, "bfloat16")
-for _n, _w in (("rma", 16), ("ua", 16), ("r2", 2), ("hc", 2), ("nl", 2), ("tk", 4), ("ib", 12), ("ibc", 12), ("vl", 1), ("hcol", 1),
-               ("df", 1), ("e0", 1), ("e4", 1), ("off", 3), ("rm1", 1024), ("rm2", 1024), ("nf", 16), ("pt0", 24), ("pt1", 24), ("pt2", 24),
-               ("tf", 2), ("q1", 2), ("q2", 2), ("pf", 2), ("wt", 208), ("wno", 192), ("ysb", 192), ("db", 512), ("dq", 576), ("g3", 192)):
+for _n, _w in (("rma", 16), ("ua", 16), ("r2", 2), ("hc", 2), ("nl", 2), ("tk", 4), ("ib", 12), ("vl", 1), ("hcol", 1),
+               ("df", 1), ("e0", 1), ("e4", 1), ("off", 2), ("rm1", 1024), ("rm2", 1024), ("n1a", 16), ("n1c", 16), ("n2a", 16), ("n2c", 16),
+               ("pf", 16), ("tf", 2), ("q1", 2), ("wt", 208), ("wno", 192), ("ysl", 208), ("ysb", 192), ("db", 512), ("dq", 576), ("g3", 192)):
     SCRATCH[_n] = _sb(_w, "float32")
 for _n, _w in (("pi", 1), ("pa", 1), ("pb", 1), ("gi", 1), ("ui", 1), ("ti", 1), ("hi", 1), ("vi", 2), ("ai", 2), ("bi", 2)):
     SCRATCH[_n] = _sb(_w, "int32")
-for _n, _w in (("zl", 12), ("zl2", 4), ("pl", 12), ("l1", 12), ("l2", 12), ("l2b", 4), ("ofo", 4), ("ofa", 12)):
+for _n, _w in (("zl", 12), ("zl2", 4), ("pl", 12), ("l1", 12), ("l2", 12), ("l2b", 4), ("ofo", 2), ("ofa", 8)):
     SCRATCH[_n] = _sb(_w, "uint16")
 for _n in ("psa", "psb", "psc", "psd", "pd0", "pd1", "pd2", "pd3"):
     SCRATCH[_n] = ("psum", [128, 512], "float32")
@@ -115,12 +115,15 @@ def rank_program(g, core, T, topo):
         need("t", *deps)
         return done("t", TE.matmul_mx(out, T[name][:, c0:c1], T[name + "s"][:, c0:c1], T[mov][:, m0:m1], T[mov + "s"][:, m0:m1], start, stop))
 
-    def pick(dst, d0, d1, win, w1, lst, *deps):
+    def pick_codes(dst, d0, d1, win, w1, lst, *deps):
         need("v", *deps)
-        need("s", *deps)
-        cv = done("v", V.tensor_copy(T[dst][:, d0:d1].bitcast(dt.uint32), T[win][:, 0:w1].bitcast(dt.uint32).indirect(lst)))
-        cs = done("s", SC.activation(T[dst + "s"][:, d0:d1], T[win + "s"][:, 0:w1].indirect(lst), F.Copy))
-        return cv, cs
+        return done("v", V.tensor_copy(T[dst][:, d0:d1].bitcast(dt.uint32), T[win][:, 0:w1].bitcast(dt.uint32).indirect(lst)))
+
+    def pick_scales(dst, d0, d1, win, w1, lst, *deps):
+        return act(T[dst + "s"][:, d0:d1], T[win + "s"][:, 0:w1].indirect(lst), F.Copy, *deps)
+
+    def pick(*a):
+        return pick_codes(*a), pick_scales(*a)
 
     peers = [T.cores[(rank + 1 + a) % NR] for a in range(3)]
     emask = _mask(topo, core, peers)
@@ -137,12 +140,12 @@ def rank_program(g, core, T, topo):
             left[0] += len(emask[c])
         g.remote_dma_fused(tr, local_sem=S["left"])
 
-    def fan_codes(src, dst, sem, c):
+    def fan_codes(src, dst, sem, *c):
         fan([T[src][:, 48 * a:48 * a + 48].bitcast(dt.uint8) for a in range(3)],
-            [T[dst][:, 48 * (2 - a):48 * (2 - a) + 48].bitcast(dt.uint8) for a in range(3)], sem, c)
+            [T[dst][:, 48 * (2 - a):48 * (2 - a) + 48].bitcast(dt.uint8) for a in range(3)], sem, *c)
 
-    def fan_scales(src, dst, sem, c):
-        fan([T[src + "s"][:, 48 * a:48 * a + 48] for a in range(3)], [T[dst + "s"][:, 48 * (2 - a):48 * (2 - a) + 48] for a in range(3)], sem, c)
+    def fan_scales(src, dst, sem, *c):
+        fan([T[src + "s"][:, 48 * a:48 * a + 48] for a in range(3)], [T[dst + "s"][:, 48 * (2 - a):48 * (2 - a) + 48] for a in range(3)], sem, *c)
 
     dma("y", T.xb[:], T.x[:], "dx")
     dma("s", T.cb[:, 0:4 * NR], T.co[:, 0:4 * NR], "dco")
@@ -160,12 +163,14 @@ def rank_program(g, core, T, topo):
     ts(T.ti[:], T.pi[:], 3 if rank < 2 else 0, None, A.bitwise_and, None)
     c = tt(T.df[:], T.gi[:], T.ui[:], A.subtract, c)
     c_tr = fill(T.trb[:, 2:516:4], 0.0, c_tr)
-    ts(T.e0[:], T.df[:], 0.0, None, A.is_equal, None, c)
-    c = ts(T.e4[:], T.df[:], 4.0, None, A.is_equal, None)
+    if rank % 2 == 0:
+        ts(T.e0[:], T.df[:], 0.0, None, A.is_equal, None, c)
+    c = ts(T.e4[:], T.df[:], 4.0, None, A.is_equal, None, c)
     c_rm = fill(T.rma[:], LOW)
-    for k, v in enumerate(((-16.0, -16.0, -12.0), (-8.0, -8.0, -4.0))[rank % 2]):
-        c = ts(T.off[:, k:k + 1], T.ti[:], v, (T.e4 if k else T.e0)[:], A.add, A.mult, c)
-    c_of = ts(T.ofo[:, 0:3], T.off[:], 16.0, None, A.add, None, c)
+    for k, (e, v) in enumerate((((T.e0, -8.0), (T.e4, -8.0)), ((T.e4, -4.0),))[rank % 2]):
+        c = ts(T.off[:, k:k + 1], T.ti[:], v, e[:], A.add, A.mult, c)
+    wide = 2 - rank % 2
+    c_of = ts(T.ofo[:, 0:wide], T.off[:, 0:wide], 8.0, None, A.add, None, c)
     c_cb = fill(T.cb[:, 4 * NR:512], 0.0)
     need("g", c_t1, c_tr)
     c_tri = done("g", g.affine_select(T.trb[:, 1:513:4], T.t1[:], [[1, 128]], A.not_equal, 1024.0, 0, -1))
@@ -177,10 +182,10 @@ def rank_program(g, core, T, topo):
     c_ib = done("g", g.iota(T.ib[:], [[256, 4], [16, 3]], 1024, 0, allow_small_or_imprecise_dtypes=True))
     need("g", c_ep0)
     c_ep = done("g", g.affine_select(T.epb[:, 4:516:4], T.on1[:], [[1, 128]], A.is_equal, 0.0, 0, -1))
-    own = slice(3 * rank, 3 * rank + 3)
-    fan([T.ofo[:, 0:3]] * 3, [T.ofa[:, own]] * 3, "oin", c_of)
+    own = slice(2 * rank, 2 * rank + wide)
+    fan([T.ofo[:, 0:wide]] * 3, [T.ofa[:, own]] * 3, "oin", c_of)
     need("y", c_of)
-    dma("y", T.ofa[:, own], T.ofo[:, 0:3], "do")
+    dma("y", T.ofa[:, own], T.ofo[:, 0:wide], "do")
 
     for k, b in enumerate((T.bm1, T.bm2)):
         for h in range(4):
@@ -191,10 +196,11 @@ def rank_program(g, core, T, topo):
         for h in range(4):
             dma("y", b[32 * h:32 * h + 32, 512 * h:512 * h + 512], (T.b1, T.b2)[k][32 * h:32 * h + 32, :], ("db1", "db2")[k])
     dma("y", T.wb[:], T.w[:], "dw")
+    c_w0 = act(T.wlb[:], T.zz[:, 0:512], F.Copy)
 
-    c_q = quant(T.cq[:], T.cqs[:], T.cb[:], ("dco", 16), c_cb)
     for k in range(2):
         quant(T.trq[:, 128 * k:128 * k + 128], T.trqs[:, 128 * k:128 * k + 128], T.trb[:, 1 - k:513 - k], c_tri)
+    c_q = quant(T.cq[:], T.cqs[:], T.cb[:], ("dco", 16), c_cb)
     c_x = quant(T.xq[:], T.xqs[:], T.xb[:], ("dx", 16))
     ts(T.pa[:], T.pi[:], 112, None, A.bitwise_and, None)
     ts(T.pb[:], T.pi[:], 15, None, A.bitwise_and, None)
@@ -217,7 +223,7 @@ def rank_program(g, core, T, topo):
     copy(T.tk[:, 1:2], T.pb[:])
     ts(T.tk[:, 2:3], T.pa[:], 64.0, T.vl[:], A.add, A.mult)
     c_tk = ts(T.tk[:, 3:4], T.pb[:], T.vl[:], None, A.mult, None)
-    c_ib = ts(T.ibc[:], T.ib[:], RND, None, A.add, None, c_ib)
+    c_ib = ts(T.ib[:], T.ib[:], RND, None, A.add, None, c_ib)
     m0 = mm(T.psc[:, 0:128], "trq", 0, 128, "otq", 0, 128, True, True, c_o)
     m1 = mm(T.psd[:, 0:128], "trq", 128, 256, "otq", 0, 128, True, True)
     need("v", m0)
@@ -229,7 +235,7 @@ def rank_program(g, core, T, topo):
     for s in range(2):
         c_nl.append(ts(T.nl[:, s:s + 1], T.hc[:, s:s + 1], RND, T.r2[:, s:s + 1], A.subtract, A.subtract, c_hcv))
     for t in range(4):
-        ts(T.ab[:, 512 + t:560:4], T.ibc[:], T.hc[:, t // 2:t // 2 + 1], T.tk[:, t:t + 1], A.is_equal, A.mult, c_tk, c_ib)
+        ts(T.ab[:, 512 + t:560:4], T.ib[:], T.hc[:, t // 2:t // 2 + 1], T.tk[:, t:t + 1], A.is_equal, A.mult, c_tk, c_ib)
     for t in range(4):
         c_a = ts(T.ab[:, t:512:4], T.im[:], T.nl[:, t // 2:t // 2 + 1], 0.0, A.add, A.is_equal, c_nl[t // 2], c_im)
     c_a = quant(T.abq[:], T.abqs[:], T.ab[:], c_a)
@@ -248,113 +254,124 @@ def rank_program(g, core, T, topo):
     for b in range(4):
         c_e = quant(T.epq[:, 128 * b:128 * b + 128], T.epqs[:, 128 * b:128 * b + 128], T.epb[:, 4 - b:516 - b], c_ep)
     c_p1 = quant(T.p1q[:], T.p1qs[:], T.pb1[:], ("dp1", 16))
+    act(T.xa[:, 64:544], T.zz[:, 0:480], F.Copy)
     for b in range(4):
         m = mm(T["pd%d" % b][:, 0:128], "epq", 128 * b, 128 * b + 128, "p1q", 0, 128, True, True, c_p1)
         need("s", m)
         c_db = done("s", SC.activation(T.db[:, 128 * b:128 * b + 128], T["pd%d" % b][:, 0:128], F.Copy, scale=-1.0))
+    act(T.xc[:, 32:528], T.zz[:, 0:496], F.Copy)
+    c_xz = act(T.xp[:, 96:560], T.zz[:, 0:464], F.Copy)
     c_b1 = quant(T.b1q[:], T.b1qs[:], T.bm1[:], ("db1", 64))
-    c_zr = fill(T.zr[:], 0.0)
-    c_w = fill(T.wlb[:], 0.0)
     c_hi = ts(T.hi[:], T.pi[:], 5, None, A.arith_shift_right, None)
-    c_zr = fill(T.zr[:, 128:129], LOW, c_zr)
     for t in range(4):
-        c_w = ts(T.wlb[:, 129 * t:128 * t + 128:4], T.im[:, 0:32], T.tk[:, 1:2], None, A.is_equal, None, c_w)
+        c_w = ts(T.wlb[:, 129 * t:128 * t + 128:4], T.im[:, 0:32], T.tk[:, 1:2], None, A.is_equal, None, c_w0)
     c_hc = ts(T.hcol[:], T.hi[:], 128.0, None, A.mult, None, c_hi)
-    for p in (T.pt0, T.pt1, T.pt2):
+    for p in (T.n1a, T.n1c, T.n2a, T.n2c, T.pf):
         c_f = fill(p[:], 0.0)
-    for p in (T.xt, T.xp):
-        fill(p[:, 96:560], 0.0)
     c_w = quant(T.wlq[:], T.wlqs[:], T.wlb[:], c_w)
+    c_b2 = quant(T.b2q[:], T.b2qs[:], T.bm2[:], ("db2", 64))
     c = ts(T.vi[:], T.r2[:], -1024.0, None, A.add, None)
     ts(T.ai[:], T.vi[:], 8, None, A.arith_shift_right, None, c)
     c = ts(T.bi[:], T.vi[:], 255, None, A.bitwise_and, None)
-    c_wt = fill(T.wt[:], -1.0)
-    c1 = ts(T.q1[:], T.ai[:], 48.0, -192.0, A.mult, A.add, c)
+    c = ts(T.q1[:], T.ai[:], 48.0, -192.0, A.mult, A.add, c)
     ts(T.tf[:], T.bi[:], 48.0, None, A.is_lt, None)
-    c = tt(T.q2[:], T.q1[:], T.bi[:], A.add, c1)
-    c = tt(T.pf[:], T.q2[:], T.tf[:], A.mult, c)
-    c = ts(T.pt0[:, 0:8:4], T.pf[:], RND, RND, A.add, A.subtract, c, c_f)
-    c_p0 = tt(T.pt0[:, 8:16:4], T.pf[:], T.pt0[:, 0:8:4], A.subtract, c)
+    c = tt(T.q1[:], T.q1[:], T.bi[:], A.add, c)
+    c_pf = tt(T.pf[:, 0:8:4], T.q1[:], T.tf[:], A.mult, c, c_f)
 
-    parts = (("psa", 0, 0, 1), ("psb", 0, 1, 1), ("psc", 0, 2, 2), ("psd", 1, 0, 2), ("pd2", 1, 2, 1), ("pd3", 1, 3, 1))
+    banks = ("psa", "psb", "psc", "psd", "pd0", "pd1", "pd2", "pd3")
 
-    def scores(tok, bk, *deps):
-        return [mm(T[b][:, 0:128 * n], tok, 64 * s, 64 * s + 128, bk, 128 * h, 128 * (h + n), True, True, *deps) for b, s, h, n in parts]
+    def scores(s, tok, c0, bk, *deps):
+        return [mm(T[banks[4 * s + h]][:, 0:128], tok, c0, c0 + 128, bk, 128 * h, 128 * h + 128, True, True, *deps) for h in range(4)]
 
-    def words(ms, rm, jk, base, pt):
-        for k, (b, s, h, n) in enumerate(parts):
+    def words(s, ms, rm, jk, nf):
+        cv = []
+        for h in range(4):
             e = 512 * s + 128 * h
-            c = scan(rm[:, e:e + 128 * n], T.zr[:, 0:128 * n], T[b][:, 0:128 * n], ms[k])
-            if k == len(parts) - 1:
-                break
-            for a in range(e, e + 128 * n, 128):
-                need("s", c)
-                cs = done("s", SC.activation(jk[:, a:a + 128], rm[:, a:a + 128], F.Sign, bias=rm[:, a + 127:a + 128], scale=-1.0,
-                                             accum_out=T.nf[:, base + a // 128:base + a // 128 + 1]))
-        c1 = ts(jk[:, e:e + 128], rm[:, e:e + 128], rm[:, e + 127:e + 128], None, A.is_lt, None, c)
-        need("v", c1)
-        cv = done("v", V.tensor_reduce(T.nf[:, base + 7:base + 8], jk[:, e:e + 128], AxisListType.X, A.add))
-        c1 = ts(pt[:, 0:8], T.nf[:, base:base + 8], RND, RND, A.add, A.subtract, cs, cv)
-        c1 = tt(pt[:, 8:16], T.nf[:, base:base + 8], pt[:, 0:8], A.subtract, c1)
-        return cs, cv, c, c1
+            cv.append(scan(rm[:, e:e + 128], T.zz[:, 0:128], T[banks[4 * s + h]][:, 0:128], ms[h]))
+            need("s", cv[-1], c_f)
+            cs = done("s", SC.activation(jk[:, e:e + 128], rm[:, e:e + 128], F.Sign, bias=rm[:, e + 127:e + 128], scale=-1.0,
+                                         accum_out=nf[:, 4 * s + h:4 * s + h + 1]))
+        return cv, cs
 
-    def spread(pt, off, xt, c1):
-        need("v", c1)
-        c = done("v", V.tensor_copy(T[xt][:, 0:96], pt[:, 0:24].indirect(off)))
+    def spread(nf, off, xt, n, *deps):
+        need("v", *deps)
+        c = done("v", V.tensor_scalar(T[xt][:, 0:n], nf[:].indirect(off), RND, RND, A.add, A.subtract))
+        need("v", c)
+        c = done("v", V.tensor_tensor(T[xt][:, n:2 * n], nf[:].indirect(off), T[xt][:, 0:n], A.subtract))
         return quant(T[xt + "q"][:], T[xt + "qs"][:], T[xt][:], c)
 
-    def tolist(bank, xt, *deps):
+    def tolist(bank, xt, w, *deps):
         mm(bank[:, 0:128], "wlq", 0, 128, xt + "q", 0, 128, True, False, *deps)
-        return mm(bank[:, 0:128], "wlq", 0, 128, xt + "q", 12, 140, False, True)
+        return mm(bank[:, 0:128], "wlq", 0, 128, xt + "q", w, 128 + w, False, True)
 
-    ms = scores("zq", "b1q", ("zin", 2 * landing), zo[0], zo[1], c_b1, c_db)
-    md = [mm(T["pd%d" % b][:, 0:192], "epq", 128 * b, 128 * b + 128, "zq", 0, 192, True, True) for b in range(2)]
-    cs, cv, c_sc, c1 = words(ms, T.rm1, T.jk1, 0, T.pt1)
-    md += [mm(T["pd%d" % b][:, 0:192], "epq", 128 * b, 128 * b + 128, "zq", 0, 192, True, True, c_sc) for b in range(2, 4)]
+    ma = scores(0, "zq", 0, "b1q", ("zin", 2 * landing), zo[0], zo[1], c_b1, c_db)
+    mc = scores(1, "zq", 64, "b1q")
+    va, sa = words(0, ma, T.rm1, T.jk1, T.n1a)
+    vc, sc = words(1, mc, T.rm1, T.jk1, T.n1c)
+
+    def unpack(b):
+        return mm(T["pd%d" % b][:, 0:192], "epq", 128 * b, 128 * b + 128, "zq", 0, 192, True, True, vc[b])
+    md = [unpack(0), unpack(1), unpack(2)]
+    ca = spread(T.n1a, T.ofa[:, 0:2], "xa", 32, sa, c_xz, ("oin", landing), ("do", 16))
+    la = tolist(T.psa, "xa", 8, ca, c_w)
+    md.append(unpack(3))
+    cc = spread(T.n1c, T.ofa[:, 2:3], "xc", 16, sc)
+    lc = tolist(T.psd, "xc", 4, cc)
+    c_d = [act(T.dq[:, 192 * b:192 * b + 192], T["pd%d" % b][:, 0:192], F.Copy, md[b]) for b in range(3)]
+    c_l = copy(T.l1[:, 0:8], T.psa[:, 0:8], la)
+    c_g = act(T.g3[:, 0:128], T.db[:, 384:512].indirect(T.l1[:, 0:8]), F.Copy, c_l)
+    need("v", c_l)
     for b in range(3):
-        c_d = act(T.dq[:, 192 * b:192 * b + 192], T["pd%d" % b][:, 0:192], F.Copy, md[b])
-    need("v", ("oin", landing), ("do", 16))
-    m = tolist(T.psa, "xt", spread(T.pt1, T.ofa[:, 0:6], "xt", c1))
-    c_b2 = quant(T.b2q[:], T.b2qs[:], T.bm2[:], ("db2", 64))
-    c_l = copy(T.l1[:], T.psa[:, 0:12], m)
-    need("s", c_l)
-    c_g3 = done("s", SC.activation(T.g3[:], T.db[:, 384:512].indirect(T.l1[:, 0:12]), F.Copy))
-    need("v", c_l, c_d, c_db)
+        need("v", c_d[b])
+        done("v", V.tensor_tensor(T.rt[:, b:512:4], T.db[:, 128 * b:128 * b + 128].indirect(T.l1[:, 0:8]), T.dq[:, 192 * b:192 * b + 128], A.add))
+    c_l = copy(T.l1[:, 8:12], T.psd[:, 0:4], lc)
+    c_g2 = act(T.g3[:, 128:192], T.db[:, 384:512].indirect(T.l1[:, 8:12]), F.Copy, c_l)
+    c = tt(T.rt[:, 3:512:4], T.g3[:, 0:128], T.pd3[:, 0:128], A.add, c_g, md[3])
+    c_r = quant(T.raq[:], T.raqs[:], T.rt[:, 0:512], c)
+    need("v", c_l)
     for b in range(3):
-        done("v", V.tensor_tensor(T.rt[:, b:768:4], T.db[:, 128 * b:128 * b + 128].indirect(T.l1[:, 0:12]), T.dq[:, 192 * b:192 * b + 192], A.add))
-    c = tt(T.rt[:, 3:768:4], T.g3[:], T.pd3[:, 0:192], A.add, c_g3, md[3])
-    c_r = quant(T.rq[:], T.rqs[:], T.rt[:], c)
-    ms = scores("rq", "b2q", c_r, c_b2)
-    vv, vs = pick("vbq", 0, 192, "p1q", 128, T.l1[:, 0:12])
+        done("v", V.tensor_tensor(T.rt[:, 512 + b:768:4], T.db[:, 128 * b:128 * b + 128].indirect(T.l1[:, 8:12]), T.dq[:, 192 * b + 128:192 * b + 192], A.add))
+    c = tt(T.rt[:, 515:768:4], T.g3[:, 128:192], T.pd3[:, 128:192], A.add, c_g2)
+    c_r2 = quant(T.rcq[:], T.rcqs[:], T.rt[:, 256:768], c)
+    ma = scores(0, "raq", 0, "b2q", c_r, c_l, c_b2)
+    mc = scores(1, "rcq", 0, "b2q", c_r2)
+    vs = pick_scales("vbq", 0, 192, "p1q", 128, T.l1[:, 0:12])
+    act(T.nbf[:, 0:4], T.n1a[:, 0:4], F.Copy)
+    act(T.nbf[:, 8:12], T.n1c[:, 4:8], F.Copy)
+    va, sa = words(0, ma, T.rm2, T.jk2, T.n2a)
+    vv = pick_codes("vbq", 0, 192, "p1q", 128, T.l1[:, 0:12])
+    vc, sc = words(1, mc, T.rm2, T.jk2, T.n2c)
     fan_scales("vbq", "lvq", "vin", vs)
     fan_codes("vbq", "lvq", "vin", vv)
     need("y", vv, vs)
     dma("y", T.lvq[:, 144:192].bitcast(dt.uint8), T.vbq[:, 144:192].bitcast(dt.uint8), "dv")
     dma("y", T.lvqs[:, 144:192], T.vbqs[:, 144:192], "dv")
-    act(T.nbf[:, 0:4], T.nf[:, 0:4], F.Copy, cs, cv)
-    act(T.nbf[:, 8:12], T.nf[:, 4:8], F.Copy)
-    cs, cv, c_sc, c1 = words(ms, T.rm2, T.jk2, 8, T.pt2)
-    act(T.nbf[:, 4:8], T.nf[:, 8:12], F.Copy, cs, cv)
-    c_nb = act(T.nbf[:, 12:16], T.nf[:, 12:16], F.Copy)
+    la = tolist(T.psa, "xa", 8, spread(T.n2a, T.ofa[:, 0:2], "xa", 32, sa))
+    lc = tolist(T.psd, "xc", 4, spread(T.n2c, T.ofa[:, 2:3], "xc", 16, sc))
+    act(T.nbf[:, 4:8], T.n2a[:, 0:4], F.Copy, sc)
+    c_nb = act(T.nbf[:, 12:16], T.n2c[:, 4:8], F.Copy)
     fan([T.nbf[:, 8 * (a // 2):8 * (a // 2) + 8] for a in range(3)], [T.ln[:, 32 * (2 - a):32 * (2 - a) + 8] for a in range(3)], "nin", c_nb)
     c_ln3 = act(T.ln[:, 96:104], T.nbf[:, 8:16], F.Copy, c_nb, c_ln)
-    m = tolist(T.psa, "xt", spread(T.pt2, T.ofa[:, 0:6], "xt", c1))
-    mp = tolist(T.psb, "xp", spread(T.pt0, T.ofa[:, 6:12], "xp", c_p0))
-    c_l = ts(T.l2[:, 0:9], T.psa[:, 0:9], T.hcol[:], None, A.add, None, m, c_hc)
-    wv, ws = pick("v2q", 0, 144, "b2q", 512, T.l2[:, 0:9], c_l)
+    c_l = ts(T.l2[:, 0:8], T.psa[:, 0:8], T.hcol[:], None, A.add, None, la, c_hc)
+    pick("v2q", 0, 128, "b2q", 512, T.l2[:, 0:8], c_l)
+    c_l = ts(T.l2[:, 8:9], T.psd[:, 0:1], T.hcol[:], None, A.add, None, lc)
+    wv, ws = pick("v2q", 128, 144, "b2q", 512, T.l2[:, 8:9], c_l)
     fan_codes("v2q", "lwq", "win", wv)
     fan_scales("v2q", "lwq", "win", ws)
-    c_l = ts(T.l2b[:, 0:3], T.psa[:, 9:12], T.hcol[:], None, A.add, None)
+    c_l = ts(T.l2b[:, 0:3], T.psd[:, 1:4], T.hcol[:], None, A.add, None)
     wo = pick("lwq", 144, 192, "b2q", 512, T.l2b[:, 0:3], c_l)
 
-    c_l = ts(T.pl[:], T.psb[:, 0:12], 192.0, None, A.add, None, mp)
+    mp = tolist(T.psb, "xp", 12, spread(T.pf, T.ofa[:, 4:7], "xp", 48, c_pf))
     c_q = quant(T.wq[:], T.wqs[:], T.wb[:], ("dw", 16))
+    c_wt = fill(T.wt[:], -1.0)
+    c_l = ts(T.pl[:], T.psb[:, 0:12], 192.0, None, A.add, None, mp)
     ov, os_ = pick("o1q", 0, 192, "lvq", 208, T.pl[:, 0:12], c_l, ("vin", 2 * landing), ("dv", 32), ("dz", 64))
     need("y", ov, os_)
     dma("y", T.oc[:, 0:768], T.o1q[:].bitcast(dt.uint8), "st")
     for k in range(4):
         dma("y", T.osc[4 * k:4 * k + 4, 0:192], T.o1qs[32 * k:32 * k + 4, :], "st")
-    mm(T.psc[:, 0:192], "wq", 0, 128, "o1q", 0, 192, True, False, ov, os_, c_q)
+    mm(T.psc[:, 0:208], "wq", 0, 128, "lvq", 0, 208, True, False, c_q, ("vin", 2 * landing), ("dv", 32), ("dz", 64))
+    m = mm(T.psc[:, 0:208], "wq", 0, 128, "lwq", 0, 208, False, True, ("win", 2 * landing), wo[0], wo[1])
     need("v", c_ln3, ("nin", landing))
     c = done("v", V.transpose(T.tr[:], T.ln[:]))
     for a, q, i, n, o in ((0, 1, 0, 32, 0), (0, 2, 0, 16, 32), (1, 1, 16, 16, 0), (1, 2, 0, 32, 16), (2, 0, 0, 32, 0), (2, 1, 0, 16, 32), (3, 2, 16, 16, 0), (3, 3, 0, 32, 16)):
@@ -364,13 +381,14 @@ def rank_program(g, core, T, topo):
     need("y", c)
     dma("y", T.wn[:], T.wno[0:8, :], "st")
     ov, os_ = pick("o2q", 0, 192, "lwq", 208, T.pl[:, 0:12], ("win", 2 * landing), wo[0], wo[1])
-    m = mm(T.psc[:, 0:192], "wq", 0, 128, "o2q", 0, 192, False, True, ov, os_)
     need("y", ov)
     dma("y", T.oc[:, 768:1536], T.o2q[:].bitcast(dt.uint8), "st")
     need("s", os_)
     for k in range(4):
         dma("s", T.osc[4 * k:4 * k + 4, 192:384], T.o2qs[32 * k:32 * k + 4, :], "st")
-    c = copy(T.ysb[:], T.psc[:, 0:192], m)
+    c = copy(T.ysl[:], T.psc[:, 0:208], m)
+    need("v", c)
+    c = done("v", V.tensor_copy(T.ysb[:], T.ysl[:].indirect(T.pl[:, 0:12])))
     need("y", c)
     dma("y", T.y[:], T.ysb[:], "st")
 

@@ -21,18 +21,18 @@ def _sb(n, d):
 
 
 SCRATCH = {}
-for _n, _w in (("xq", 192), ("cq", 128), ("wq", 128), ("p1q", 128), ("b1q", 512), ("b2q", 512), ("trq", 256), ("wlq", 128), ("epq", 512),
-               ("otq", 128), ("abq", 140), ("xaq", 136), ("xcq", 132), ("xpq", 140), ("zsq", 144), ("zq", 192), ("vbq", 192), ("lvq", 208),
+for _n, _w in (("xq", 192), ("cq", 134), ("wq", 128), ("p1q", 128), ("b1q", 512), ("b2q", 512), ("trq", 256), ("wlq", 128), ("epq", 512),
+               ("otq", 134), ("abq", 140), ("xaq", 136), ("xcq", 132), ("xpq", 140), ("zsq", 144), ("zq", 192), ("vbq", 192), ("lvq", 208),
                ("v2q", 144), ("lwq", 208), ("raq", 128), ("rcq", 128), ("o1q", 192), ("o2q", 192)):
     SCRATCH[_n] = _codes(_w)
     SCRATCH[_n + "s"] = _plane(_w)
-for _n, _w in (("xb", 768), ("cb", 512), ("wb", 512), ("pb1", 512), ("bm1", 2048), ("bm2", 2048), ("trb", 516), ("wlb", 512), ("epb", 516),
-               ("ot", 512), ("ab", 560), ("xa", 544), ("xc", 528), ("xp", 560), ("rt", 768), ("zz", 516), ("on1", 128), ("t1", 128), ("im", 128),
-               ("jk1", 1024), ("jk2", 1024), ("nbf", 16), ("ln", 128), ("tr", 128)):
+for _n, _w in (("xb", 768), ("cb", 536), ("wb", 512), ("pb1", 512), ("pb2", 512), ("bm1", 2048), ("bm2", 2048), ("trb", 516), ("wlb", 512),
+               ("epb", 516), ("ot", 536), ("ab", 560), ("xa", 544), ("xc", 528), ("xp", 560), ("rt", 768), ("zz", 536), ("on1", 128),
+               ("t1", 128), ("im", 128), ("jk1", 1024), ("jk2", 1024), ("nbf", 16), ("ln", 128), ("tr", 128)):
     SCRATCH[_n] = _sb(_w, "bfloat16")
-for _n, _w in (("rma", 16), ("ua", 16), ("r2", 2), ("hc", 2), ("nl", 2), ("tk", 4), ("ib", 12), ("vl", 1), ("hcol", 1),
-               ("df", 1), ("e0", 1), ("e4", 1), ("off", 2), ("rm1", 1024), ("rm2", 1024), ("n1a", 16), ("n1c", 16), ("n2a", 16), ("n2c", 16),
-               ("pf", 16), ("tf", 2), ("q1", 2), ("wt", 208), ("wno", 192), ("ysl", 208), ("ysb", 192), ("db", 512), ("dq", 576), ("g3", 192)):
+for _n, _w in (("rst", 10), ("rma", 10), ("ua", 11), ("rr", 10), ("hc", 2), ("nl", 2), ("tk", 4), ("tkn", 2), ("ib", 12), ("abx", 12),
+               ("vl", 1), ("mk", 4), ("hcol", 1), ("df", 1), ("e0", 1), ("e4", 1), ("off", 2), ("rm1", 1024), ("rm2", 1024), ("nf", 80),
+               ("tf", 2), ("q1", 2), ("wt", 208), ("wno", 192), ("ysb", 192), ("db", 512), ("dq", 384), ("g2", 192), ("g3", 192)):
     SCRATCH[_n] = _sb(_w, "float32")
 for _n, _w in (("pi", 1), ("pa", 1), ("pb", 1), ("gi", 1), ("ui", 1), ("ti", 1), ("hi", 1), ("vi", 2), ("ai", 2), ("bi", 2)):
     SCRATCH[_n] = _sb(_w, "int32")
@@ -40,7 +40,8 @@ for _n, _w in (("zl", 12), ("zl2", 4), ("pl", 12), ("l1", 12), ("l2", 12), ("l2b
     SCRATCH[_n] = _sb(_w, "uint16")
 for _n in ("psa", "psb", "psc", "psd", "pd0", "pd1", "pd2", "pd3"):
     SCRATCH[_n] = ("psum", [128, 512], "float32")
-SEMAPHORES = ["qv", "qs", "qt", "qg", "dx", "dco", "dp1", "db1", "db2", "dw", "dz", "dv", "do", "st", "zin", "vin", "win", "nin", "oin", "left"]
+SEMAPHORES = ["qv", "qs", "qt", "qg", "dx", "dco", "dp1", "dp2", "db2", "dep", "dw", "dz", "dv", "do", "st", "zin", "vin", "win", "nin", "oin",
+              "left"]
 
 
 def _mask(topo, src, peers):
@@ -148,247 +149,321 @@ def rank_program(g, core, T, topo):
         fan([T[src + "s"][:, 48 * a:48 * a + 48] for a in range(3)], [T[dst + "s"][:, 48 * (2 - a):48 * (2 - a) + 48] for a in range(3)], sem, *c)
 
     dma("y", T.xb[:], T.x[:], "dx")
-    dma("s", T.cb[:, 0:4 * NR], T.co[:, 0:4 * NR], "dco")
+    dma("s", T.cb[:, 24:40], T.co[:, 0:4 * NR], "dco")
+    dma("y", T.pb1[:], T.b1[:], "dp1")
 
     c_pi = done("g", g.iota(T.pi[:], [[0, 1]], 0, 1))
     c_on = fill(T.on1[:], 1.0)
     c_zz = fill(T.zz[:], 0.0)
-    c_tr = fill(T.trb[:], 1.0)
-    c_ot = act(T.ot[:], T.zz[:, 0:512], F.Copy, c_zz)
-    c_ep0 = act(T.epb[:], T.zz[:], F.Copy)
+    need("y", c_zz)
+    dma("y", T.epb[:], T.zz[:, 0:516], "dep")
+    dma("y", T.pb2[:], T.b2[:], "dp2")
+    need("s", c_zz)
+    c_tr = done("s", SC.activation(T.trb[:], T.zz[:, 0:516], F.Identity, bias=1.0))
+    c_ot = act(T.ot[:], T.zz[:], F.Copy)
     need("g", c_on)
     c_t1 = done("g", g.affine_select(T.t1[:], T.on1[:], [[1, 128]], A.is_gt, 0.0, 0, -1))
+    c_cb = done("g", g.iota(T.cb[:, 40:536], [[0, 496]], 0, 0, allow_small_or_imprecise_dtypes=True))
     ts(T.gi[:], T.pi[:], 4, None, A.arith_shift_right, None, c_pi)
     c = ts(T.ui[:], T.pi[:], 2, 3, A.arith_shift_right, A.bitwise_and)
     ts(T.ti[:], T.pi[:], 3 if rank < 2 else 0, None, A.bitwise_and, None)
+    c_hi = ts(T.hi[:], T.pi[:], 5, None, A.arith_shift_right, None)
     c = tt(T.df[:], T.gi[:], T.ui[:], A.subtract, c)
-    c_tr = fill(T.trb[:, 2:516:4], 0.0, c_tr)
+    c_cb0 = fill(T.cb[:, 0:24], 0.0)
+    for h in range(4):
+        c_mk = ts(T.mk[:, h:h + 1], T.hi[:], float(h), None, A.is_equal, None, c_hi)
     if rank % 2 == 0:
         ts(T.e0[:], T.df[:], 0.0, None, A.is_equal, None, c)
     c = ts(T.e4[:], T.df[:], 4.0, None, A.is_equal, None, c)
-    c_rm = fill(T.rma[:], LOW)
+    c_tr = fill(T.trb[:, 2:516:4], 0.0, c_tr)
     for k, (e, v) in enumerate((((T.e0, -8.0), (T.e4, -8.0)), ((T.e4, -4.0),))[rank % 2]):
         c = ts(T.off[:, k:k + 1], T.ti[:], v, e[:], A.add, A.mult, c)
     wide = 2 - rank % 2
+    c_rs = fill(T.rst[:], 0.0)
     c_of = ts(T.ofo[:, 0:wide], T.off[:, 0:wide], 8.0, None, A.add, None, c)
-    c_cb = fill(T.cb[:, 4 * NR:512], 0.0)
+    c_rs = fill(T.rst[:, 4:7], LOW, c_rs)
     need("g", c_t1, c_tr)
     c_tri = done("g", g.affine_select(T.trb[:, 1:513:4], T.t1[:], [[1, 128]], A.not_equal, 1024.0, 0, -1))
     need("g", c_ot)
-    c_ot = done("g", g.iota(T.ot[:, 3:4 * rank + 4:4], [[2, rank + 1]], 2 * (3 - rank), 0, allow_small_or_imprecise_dtypes=True))
-    if rank < NR - 1:
-        c_ot = done("g", g.iota(T.ot[:, 4 * rank + 7:16:4], [[2, NR - 1 - rank]], 0, 0, allow_small_or_imprecise_dtypes=True))
-    c_im = done("g", g.iota(T.im[:], [[0, 8], [1, 16]], 0, 0, allow_small_or_imprecise_dtypes=True))
-    c_ib = done("g", g.iota(T.ib[:], [[256, 4], [16, 3]], 1024, 0, allow_small_or_imprecise_dtypes=True))
-    need("g", c_ep0)
-    c_ep = done("g", g.affine_select(T.epb[:, 4:516:4], T.on1[:], [[1, 128]], A.is_equal, 0.0, 0, -1))
+    c_oi = done("g", g.iota(T.ot[:, 27:75:4], [[0, 2], [2, 6]], 0, 0, allow_small_or_imprecise_dtypes=True))
     own = slice(2 * rank, 2 * rank + wide)
     fan([T.ofo[:, 0:wide]] * 3, [T.ofa[:, own]] * 3, "oin", c_of)
     need("y", c_of)
     dma("y", T.ofa[:, own], T.ofo[:, 0:wide], "do")
-
-    for k, b in enumerate((T.bm1, T.bm2)):
-        for h in range(4):
-            c_z = act(b[:, 512 * h:512 * h + 512], T.zz[:, 0:512], F.Copy, c_zz)
-        need("y", c_z)
-        if k == 0:
-            dma("y", T.pb1[:], T.b1[:], "dp1")
-        for h in range(4):
-            dma("y", b[32 * h:32 * h + 32, 512 * h:512 * h + 512], (T.b1, T.b2)[k][32 * h:32 * h + 32, :], ("db1", "db2")[k])
-    dma("y", T.wb[:], T.w[:], "dw")
+    if rank < NR - 1:
+        done("g", g.iota(T.ib[:, 0:9 - 3 * rank], [[256, 3 - rank], [16, 3]], 1280 + 256 * rank, 0, allow_small_or_imprecise_dtypes=True))
+    c_ib = done("g", g.iota(T.ib[:, 9 - 3 * rank:12], [[256, rank + 1], [16, 3]], 1024, 0, allow_small_or_imprecise_dtypes=True))
+    c_im = done("g", g.iota(T.im[:], [[0, 8], [1, 16]], 0, 0, allow_small_or_imprecise_dtypes=True))
+    need("g", ("dep", 16))
+    c_ep = done("g", g.affine_select(T.epb[:, 4:516:4], T.on1[:], [[1, 128]], A.is_equal, 0.0, 0, -1))
     c_w0 = act(T.wlb[:], T.zz[:, 0:512], F.Copy)
+    c_xp = act(T.xp[:, 96:560], T.zz[:, 0:464], F.Copy)
 
-    for k in range(2):
-        quant(T.trq[:, 128 * k:128 * k + 128], T.trqs[:, 128 * k:128 * k + 128], T.trb[:, 1 - k:513 - k], c_tri)
-    c_q = quant(T.cq[:], T.cqs[:], T.cb[:], ("dco", 16), c_cb)
+    def masked(bm, pb, h):
+        return done("s", SC.activation(bm[:, 512 * h:512 * h + 512], pb[:], F.Copy, scale=T.mk[:, h:h + 1]))
+    need("s", c_mk, ("dp1", 16))
+    for h in range(3):
+        masked(T.bm1, T.pb1, h)
+
+    c_q = quant(T.cq[:], T.cqs[:], T.cb[:], ("dco", 16), c_cb, c_cb0)
     c_x = quant(T.xq[:], T.xqs[:], T.xb[:], ("dx", 16))
-    ts(T.pa[:], T.pi[:], 112, None, A.bitwise_and, None)
-    ts(T.pb[:], T.pi[:], 15, None, A.bitwise_and, None)
-    c_vl = ts(T.vl[:], T.pi[:], 64.0, None, A.is_ge, None)
-    c_ln = fill(T.ln[:], 0.0)
-    m0 = mm(T.psa[:, 0:128], "xq", 0, 128, "cq", 0, 128, True, True, c_x)
-    m1 = mm(T.psb[:, 0:128], "xq", 64, 192, "cq", 0, 128, True, True)
-
-    def scan(out, d0, d1, *deps):
-        need("v", *deps)
-        return done("v", V.tensor_tensor_scan(out, d0, d1, LOW, A.add, A.max))
-    s0 = scan(T.rma[:, 1:5], T.zz[:, 0:4], T.psa[:, 0:4], m0, c_rm)
-    s1 = scan(T.rma[:, 9:13], T.zz[:, 0:4], T.psb[:, 0:4], m1)
-    u0 = ts(T.ua[:, 0:5], T.rma[:, 0:5], T.rma[:, 4:5], None, A.is_equal, None, s0)
-    u1 = ts(T.ua[:, 8:13], T.rma[:, 8:13], T.rma[:, 12:13], T.vl[:], A.is_equal, A.mult, s1, c_vl)
-    tt(T.ot[:, 0:16:4], T.ua[:, 1:5], T.ua[:, 0:4], A.subtract, u0, c_ot)
-    o1 = tt(T.ot[:, 1:16:4], T.ua[:, 9:13], T.ua[:, 8:12], A.subtract, u1)
-    c_o = quant(T.otq[:], T.otqs[:], T.ot[:], o1)
-    copy(T.tk[:, 0:1], T.pa[:])
-    copy(T.tk[:, 1:2], T.pb[:])
-    ts(T.tk[:, 2:3], T.pa[:], 64.0, T.vl[:], A.add, A.mult)
-    c_tk = ts(T.tk[:, 3:4], T.pb[:], T.vl[:], None, A.mult, None)
-    c_ib = ts(T.ib[:], T.ib[:], RND, None, A.add, None, c_ib)
-    m0 = mm(T.psc[:, 0:128], "trq", 0, 128, "otq", 0, 128, True, True, c_o)
-    m1 = mm(T.psd[:, 0:128], "trq", 128, 256, "otq", 0, 128, True, True)
-    need("v", m0)
-    done("v", V.tensor_reduce(T.r2[:, 0:1], T.psc[:, 0:4], AxisListType.X, A.max))
-    need("v", m1)
-    r = done("v", V.tensor_reduce(T.r2[:, 1:2], T.psd[:, 0:4], AxisListType.X, A.max))
-    c_hcv = ts(T.hc[:], T.r2[:], -7.5, RND, A.add, A.add, r)
-    c_nl = []
-    for s in range(2):
-        c_nl.append(ts(T.nl[:, s:s + 1], T.hc[:, s:s + 1], RND, T.r2[:, s:s + 1], A.subtract, A.subtract, c_hcv))
-    for t in range(4):
-        ts(T.ab[:, 512 + t:560:4], T.ib[:], T.hc[:, t // 2:t // 2 + 1], T.tk[:, t:t + 1], A.is_equal, A.mult, c_tk, c_ib)
-    for t in range(4):
-        c_a = ts(T.ab[:, t:512:4], T.im[:], T.nl[:, t // 2:t // 2 + 1], 0.0, A.add, A.is_equal, c_nl[t // 2], c_im)
-    c_a = quant(T.abq[:], T.abqs[:], T.ab[:], c_a)
-    m0 = mm(T.psa[:, 0:128], "abq", 0, 128, "abq", 12, 140, True, True, c_a)
-    c_l = copy(T.zl[:, 0:9], T.psa[:, 116:125], m0)
-    zv, zs = pick("zsq", 0, 144, "xq", 192, T.zl[:, 0:9], c_l)
-    fan_codes("zsq", "zq", "zin", zv)
-    fan_scales("zsq", "zq", "zin", zs)
-    c_l = copy(T.zl2[:, 0:3], T.psa[:, 125:128])
-    zo = pick("zq", 144, 192, "xq", 192, T.zl2[:, 0:3], c_l)
     need("y", c_q)
     for b in ("lvq", "lwq"):
         dma("y", T[b][:, 192:208].bitcast(dt.uint8), T.cq[:, 64:80].bitcast(dt.uint8), "dz")
         dma("y", T[b + "s"][:, 192:208], T.cqs[:, 64:80], "dz")
+    mm(T.psa[:, 0:128], "xq", 0, 128, "cq", 6, 134, True, False, c_x)
+    m = mm(T.psa[:, 0:128], "xq", 64, 192, "cq", 0, 128, False, True)
+    c_ua = fill(T.ua[:], 0.0)
+    c_vl = ts(T.vl[:], T.pi[:], 64.0, None, A.is_ge, None)
+    c_o1 = fill(T.ot[:, 1:64:4], -7.5 / 128, c_ot)
+    for k in range(2):
+        quant(T.trq[:, 128 * k:128 * k + 128], T.trqs[:, 128 * k:128 * k + 128], T.trb[:, 1 + 2 * k:513 + 2 * k], c_tri)
 
-    for b in range(4):
-        c_e = quant(T.epq[:, 128 * b:128 * b + 128], T.epqs[:, 128 * b:128 * b + 128], T.epb[:, 4 - b:516 - b], c_ep)
+    def scan(out, d0, d1, *deps):
+        need("v", *deps)
+        return done("v", V.tensor_tensor_scan(out, d0, d1, LOW, A.add, A.max))
+    s = scan(T.rma[:], T.rst[:], T.psa[:, 0:10], m, c_rs)
+    ts(T.pa[:], T.pi[:], 112, None, A.bitwise_and, None)
+    u = ts(T.ua[:, 1:5], T.rma[:, 0:4], T.rma[:, 3:4], None, A.is_equal, None, s, c_ua)
+    u = ts(T.ua[:, 7:11], T.rma[:, 6:10], T.rma[:, 9:10], T.vl[:], A.is_equal, A.mult, c_vl)
+    c_pb = ts(T.pb[:], T.pi[:], 15, None, A.bitwise_and, None)
+    o = tt(T.ot[:, 24:64:4], T.ua[:, 1:11], T.ua[:, 0:10], A.subtract, u, c_o1)
+    c_o = quant(T.otq[:], T.otqs[:], T.ot[:], o, c_oi)
+    mm(T.psc[:, 0:128], "trq", 0, 128, "otq", 6, 134, True, False, c_o)
+    m = mm(T.psc[:, 0:128], "trq", 128, 256, "otq", 0, 128, False, True)
+    ts(T.tk[:, 2:3], T.pa[:], 64.0, T.vl[:], A.add, A.mult, c_pb)
+    c = ts(T.tk[:, 3:4], T.pb[:], T.vl[:], None, A.mult, None)
+    copy(T.tk[:, 0:1], T.pa[:])
+    c_tk = copy(T.tk[:, 1:2], T.pb[:])
+    c_tn = ts(T.tkn[:], T.tk[:, 2:4], -0.0625, None, A.mult, None, c)
+    c_ln = fill(T.ln[:], 0.0)
+    r = scan(T.rr[:], T.rst[:], T.psc[:, 0:10], m)
+    c_hc = ts(T.hc[:], T.rr[:, 3:10:6], RND, RND, A.add, A.subtract, r)
+    need("s", c_hc, c_ib, c_tn)
+    c = done("s", SC.activation(T.abx[:], T.ib[:], F.Abs, bias=T.hc[:, 1:2], scale=-1.0))
+    need("s", c)
+    for t in (2, 3):
+        c_b = done("s", SC.activation(T.ab[:, 512 + t:560:4], T.abx[:], F.Relu, bias=T.tk[:, t:t + 1], scale=T.tkn[:, t - 2:t - 1]))
+    c_m1 = masked(T.bm1, T.pb1, 3)
+    c_nl = tt(T.nl[:], T.hc[:], T.rr[:, 3:10:6], A.subtract, c_hc)
+    for t in range(2):
+        ts(T.ab[:, 512 + t:560:4], T.ib[:], T.hc[:, 0:1], T.tk[:, t:t + 1], A.is_equal, A.mult, c_tk, c_ib)
+    for t in range(4):
+        c_a = ts(T.ab[:, t:512:4], T.im[:], T.nl[:, t // 2:t // 2 + 1], 7.5, A.subtract, A.is_equal, c_nl, c_im) if False else \
+            ts(T.ab[:, t:512:4], T.im[:], T.nl[:, t // 2:t // 2 + 1], 7.5, A.add, A.is_equal, c_nl, c_im)
+    c_a = quant(T.abq[:], T.abqs[:], T.ab[:], c_a, c_b)
+    m0 = mm(T.psa[:, 0:128], "abq", 0, 128, "abq", 12, 140, True, True, c_a)
+
+    def e_tile(b):
+        return quant(T.epq[:, 128 * b:128 * b + 128], T.epqs[:, 128 * b:128 * b + 128], T.epb[:, 4 - b:516 - b], c_ep)
+    c_e = [e_tile(0), e_tile(1)]
+    c_l = copy(T.zl[:, 0:9], T.psa[:, 116:125], m0)
+    zv, zs = pick("zsq", 0, 144, "xq", 192, T.zl[:, 0:9], c_l)
+    fan_codes("zsq", "zq", "zin", zv, c_ln)
+    fan_scales("zsq", "zq", "zin", zs)
+    c_l = copy(T.zl2[:, 0:3], T.psa[:, 125:128])
     c_p1 = quant(T.p1q[:], T.p1qs[:], T.pb1[:], ("dp1", 16))
-    act(T.xa[:, 64:544], T.zz[:, 0:480], F.Copy)
-    for b in range(4):
-        m = mm(T["pd%d" % b][:, 0:128], "epq", 128 * b, 128 * b + 128, "p1q", 0, 128, True, True, c_p1)
+    zo = pick("zq", 144, 192, "xq", 192, T.zl2[:, 0:3], c_l)
+
+    c_xc = done("g", g.iota(T.xc[:, 32:528], [[0, 496]], 0, 0, allow_small_or_imprecise_dtypes=True))
+    for h in range(2):
+        c_g = done("g", g.iota(T.bm2[:, 512 * h:512 * h + 512], [[0, 512]], 0, 0, allow_small_or_imprecise_dtypes=True))
+    need("y", c_g)
+    for h in range(2):
+        dma("y", T.bm2[32 * h:32 * h + 32, 512 * h:512 * h + 512], T.b2[32 * h:32 * h + 32, :], "db2")
+    dma("y", T.wb[:], T.w[:], "dw")
+    c_db = []
+
+    def table(b):
+        m = mm(T["pd%d" % b][:, 0:128], "epq", 128 * b, 128 * b + 128, "p1q", 0, 128, True, True, c_e[b], c_p1)
         need("s", m)
-        c_db = done("s", SC.activation(T.db[:, 128 * b:128 * b + 128], T["pd%d" % b][:, 0:128], F.Copy, scale=-1.0))
-    act(T.xc[:, 32:528], T.zz[:, 0:496], F.Copy)
-    c_xz = act(T.xp[:, 96:560], T.zz[:, 0:464], F.Copy)
-    c_b1 = quant(T.b1q[:], T.b1qs[:], T.bm1[:], ("db1", 64))
-    c_hi = ts(T.hi[:], T.pi[:], 5, None, A.arith_shift_right, None)
+        c_db.append(done("s", SC.activation(T.db[:, 128 * b:128 * b + 128], T["pd%d" % b][:, 0:128], F.Copy, scale=-1.0)))
+    table(0)
+    table(1)
+    c_xa = act(T.xa[:, 64:544], T.zz[:, 0:480], F.Copy)
+    c_e.append(e_tile(2))
+    c_e.append(e_tile(3))
+    table(2)
+    table(3)
+    c_b1 = quant(T.b1q[:], T.b1qs[:], T.bm1[:], c_m1)
+    need("s", ("dp2", 16))
+    for h in (2, 3):
+        c_m2 = masked(T.bm2, T.pb2, h)
+    c_f = fill(T.nf[:], 0.0)
     for t in range(4):
         c_w = ts(T.wlb[:, 129 * t:128 * t + 128:4], T.im[:, 0:32], T.tk[:, 1:2], None, A.is_equal, None, c_w0)
-    c_hc = ts(T.hcol[:], T.hi[:], 128.0, None, A.mult, None, c_hi)
-    for p in (T.n1a, T.n1c, T.n2a, T.n2c, T.pf):
-        c_f = fill(p[:], 0.0)
+    c = ts(T.vi[:], T.rr[:, 3:10:6], -1016.5 + 256 * (3 - rank), None, A.add, None)
     c_w = quant(T.wlq[:], T.wlqs[:], T.wlb[:], c_w)
-    c_b2 = quant(T.b2q[:], T.b2qs[:], T.bm2[:], ("db2", 64))
-    c = ts(T.vi[:], T.r2[:], -1024.0, None, A.add, None)
-    ts(T.ai[:], T.vi[:], 8, None, A.arith_shift_right, None, c)
-    c = ts(T.bi[:], T.vi[:], 255, None, A.bitwise_and, None)
-    c = ts(T.q1[:], T.ai[:], 48.0, -192.0, A.mult, A.add, c)
-    ts(T.tf[:], T.bi[:], 48.0, None, A.is_lt, None)
-    c = tt(T.q1[:], T.q1[:], T.bi[:], A.add, c)
-    c_pf = tt(T.pf[:, 0:8:4], T.q1[:], T.tf[:], A.mult, c, c_f)
+    ts(T.ai[:], T.vi[:], 8, 3, A.arith_shift_right, A.bitwise_and, c)
+    c_bi = ts(T.bi[:], T.vi[:], 255, None, A.bitwise_and, None)
+    c_hcol = ts(T.hcol[:], T.hi[:], 128.0, None, A.mult, None)
 
-    banks = ("psa", "psb", "psc", "psd", "pd0", "pd1", "pd2", "pd3")
+    where = ((("psa", 0), ("psb", 0), ("psc", 0), ("psc", 128)), (("psd", 0), ("psd", 128), ("psd", 256), ("psd", 384)),
+             (("pd0", 0), ("pd1", 0), ("pd2", 0), ("pd3", 0)))
+    N1A, N1C, N2A, N2C, NP = 0, 16, 32, 48, 64
+    O0, O1, OP = T.ofa[:, 0:2], T.ofa[:, 2:3], T.ofa[:, 4:7]
 
-    def scores(s, tok, c0, bk, *deps):
-        return [mm(T[banks[4 * s + h]][:, 0:128], tok, c0, c0 + 128, bk, 128 * h, 128 * h + 128, True, True, *deps) for h in range(4)]
+    def scores(k, tok, c0, bk, *deps):
+        if k == 2:
+            return [mm(T["pd%d" % h][:, 0:128], tok, c0, c0 + 128, bk, 128 * h, 128 * h + 128, True, True, *deps) for h in range(4)]
+        if k == 1:
+            return [mm(T.psd[:, 0:512], tok, c0, c0 + 128, bk, 0, 512, True, True, *deps)] * 4
+        m = [mm(T[("psa", "psb")[h]][:, 0:128], tok, c0, c0 + 128, bk, 128 * h, 128 * h + 128, True, True, *deps) for h in range(2)]
+        return m + [mm(T.psc[:, 0:256], tok, c0, c0 + 128, bk, 256, 512, True, True)] * 2
 
-    def words(s, ms, rm, jk, nf):
-        cv = []
-        for h in range(4):
-            e = 512 * s + 128 * h
-            cv.append(scan(rm[:, e:e + 128], T.zz[:, 0:128], T[banks[4 * s + h]][:, 0:128], ms[h]))
-            need("s", cv[-1], c_f)
-            cs = done("s", SC.activation(jk[:, e:e + 128], rm[:, e:e + 128], F.Sign, bias=rm[:, e + 127:e + 128], scale=-1.0,
-                                         accum_out=nf[:, 4 * s + h:4 * s + h + 1]))
-        return cv, cs
+    def word(k, h, m, rm, jk, at):
+        s = min(k, 1)
+        e = 512 * s + 128 * h
+        b, o = where[k][h]
+        cv = scan(rm[:, e:e + 128], T.zz[:, 0:128], T[b][:, o:o + 128], m[h])
+        need("s", cv, c_f)
+        return cv, done("s", SC.activation(jk[:, e:e + 128], rm[:, e:e + 128], F.Sign, bias=rm[:, e + 127:e + 128], scale=-1.0,
+                                           accum_out=T.nf[:, at + 4 * s + h:at + 4 * s + h + 1]))
 
-    def spread(nf, off, xt, n, *deps):
+    def part_hi(at, off, xt, n, *deps):
         need("v", *deps)
-        c = done("v", V.tensor_scalar(T[xt][:, 0:n], nf[:].indirect(off), RND, RND, A.add, A.subtract))
+        return done("v", V.tensor_scalar(T[xt][:, 0:n], T.nf[:, at:at + 16].indirect(off), RND, RND, A.add, A.subtract))
+
+    def part_lo(at, off, xt, n, c):
         need("v", c)
-        c = done("v", V.tensor_tensor(T[xt][:, n:2 * n], nf[:].indirect(off), T[xt][:, 0:n], A.subtract))
+        return done("v", V.tensor_tensor(T[xt][:, n:2 * n], T.nf[:, at:at + 16].indirect(off), T[xt][:, 0:n], A.subtract))
+
+    def part_q(xt, c):
         return quant(T[xt + "q"][:], T[xt + "qs"][:], T[xt][:], c)
 
     def tolist(bank, xt, w, *deps):
         mm(bank[:, 0:128], "wlq", 0, 128, xt + "q", 0, 128, True, False, *deps)
         return mm(bank[:, 0:128], "wlq", 0, 128, xt + "q", w, 128 + w, False, True)
 
-    ma = scores(0, "zq", 0, "b1q", ("zin", 2 * landing), zo[0], zo[1], c_b1, c_db)
-    mc = scores(1, "zq", 64, "b1q")
-    va, sa = words(0, ma, T.rm1, T.jk1, T.n1a)
-    vc, sc = words(1, mc, T.rm1, T.jk1, T.n1c)
+    def book2(h, *deps):
+        return quant(T.b2q[:, 128 * h:128 * h + 128], T.b2qs[:, 128 * h:128 * h + 128], T.bm2[:, 512 * h:512 * h + 512], *deps)
 
     def unpack(b):
-        return mm(T["pd%d" % b][:, 0:192], "epq", 128 * b, 128 * b + 128, "zq", 0, 192, True, True, vc[b])
-    md = [unpack(0), unpack(1), unpack(2)]
-    ca = spread(T.n1a, T.ofa[:, 0:2], "xa", 32, sa, c_xz, ("oin", landing), ("do", 16))
-    la = tolist(T.psa, "xa", 8, ca, c_w)
-    md.append(unpack(3))
-    cc = spread(T.n1c, T.ofa[:, 2:3], "xc", 16, sc)
-    lc = tolist(T.psd, "xc", 4, cc)
-    c_d = [act(T.dq[:, 192 * b:192 * b + 192], T["pd%d" % b][:, 0:192], F.Copy, md[b]) for b in range(3)]
+        return mm(T["pd%d" % b][:, 0:192], "epq", 128 * b, 128 * b + 128, "zq", 0, 192, True, True, c_db[b])
+
+    ma = scores(0, "zq", 0, "b1q", ("zin", 2 * landing), zo[0], zo[1], c_b1)
+    mc = scores(1, "zq", 64, "b1q")
+    md = [unpack(b) for b in range(4)]
+    word(0, 0, ma, T.rm1, T.jk1, N1A)
+    cq1 = ts(T.q1[:], T.ai[:], 48.0, -192.0, A.mult, A.add, c_bi)
+    word(0, 1, ma, T.rm1, T.jk1, N1A)
+    ts(T.tf[:], T.bi[:], 48.0, None, A.is_lt, None)
+    cq1 = tt(T.q1[:], T.q1[:], T.bi[:], A.add, cq1)
+    word(0, 2, ma, T.rm1, T.jk1, N1A)
+    c_pf = tt(T.nf[:, 64:72:4], T.q1[:], T.tf[:], A.mult, cq1, c_f)
+    _, sa = word(0, 3, ma, T.rm1, T.jk1, N1A)
+    cx = part_hi(NP, OP, "xp", 48, c_pf, c_xp, ("oin", landing), ("do", 16))
+    word(1, 0, mc, T.rm1, T.jk1, N1C)
+    cx = part_lo(NP, OP, "xp", 48, cx)
+    word(1, 1, mc, T.rm1, T.jk1, N1C)
+    c = part_hi(N1A, O0, "xa", 32, sa, c_xa)
+    word(1, 2, mc, T.rm1, T.jk1, N1C)
+    c = part_lo(N1A, O0, "xa", 32, c)
+    _, sc = word(1, 3, mc, T.rm1, T.jk1, N1C)
+    c = part_q("xa", c)
+    la = tolist(T.psa, "xa", 8, c, c_w)
+    cx = part_q("xp", cx)
+    c = part_hi(N1C, O1, "xc", 16, sc, c_xc)
+    book2(2, c_m2)
+    c = part_lo(N1C, O1, "xc", 16, c)
+    book2(3)
+    c = part_q("xc", c)
+    lc = tolist(T.psb, "xc", 4, c)
+    mp = tolist(T.psd, "xp", 12, cx)
+    c_d = [act(T.dq[:, 192 * b:192 * b + 192], T["pd%d" % b][:, 0:192], F.Copy, md[b]) for b in range(2)]
+
+    def rest_gather(d0, d1, lst, c):
+        need("v", c)
+        for b in range(2):
+            need("v", c_d[b])
+            done("v", V.tensor_tensor(T.rt[:, 4 * d0 + b:4 * d1:4], T.db[:, 128 * b:128 * b + 128].indirect(lst), T.dq[:, 192 * b + d0:192 * b + d1], A.add))
+        return [act(T["g%d" % b][:, d0:d1], T.db[:, 128 * b:128 * b + 128].indirect(lst), F.Copy, c) for b in (2, 3)]
+
+    def rest_add(d0, d1, cg):
+        for b in (2, 3):
+            c = tt(T.rt[:, 4 * d0 + b:4 * d1:4], T["g%d" % b][:, d0:d1], T["pd%d" % b][:, d0:d1], A.add, cg[b - 2], md[b])
+        return c
     c_l = copy(T.l1[:, 0:8], T.psa[:, 0:8], la)
-    c_g = act(T.g3[:, 0:128], T.db[:, 384:512].indirect(T.l1[:, 0:8]), F.Copy, c_l)
-    need("v", c_l)
-    for b in range(3):
-        need("v", c_d[b])
-        done("v", V.tensor_tensor(T.rt[:, b:512:4], T.db[:, 128 * b:128 * b + 128].indirect(T.l1[:, 0:8]), T.dq[:, 192 * b:192 * b + 128], A.add))
-    c_l = copy(T.l1[:, 8:12], T.psd[:, 0:4], lc)
-    c_g2 = act(T.g3[:, 128:192], T.db[:, 384:512].indirect(T.l1[:, 8:12]), F.Copy, c_l)
-    c = tt(T.rt[:, 3:512:4], T.g3[:, 0:128], T.pd3[:, 0:128], A.add, c_g, md[3])
+    cg = rest_gather(0, 128, T.l1[:, 0:8], c_l)
+    c_l = copy(T.l1[:, 8:12], T.psb[:, 0:4], lc)
+    book2(0, ("db2", 32))
+    c = rest_add(0, 128, cg)
     c_r = quant(T.raq[:], T.raqs[:], T.rt[:, 0:512], c)
-    need("v", c_l)
-    for b in range(3):
-        done("v", V.tensor_tensor(T.rt[:, 512 + b:768:4], T.db[:, 128 * b:128 * b + 128].indirect(T.l1[:, 8:12]), T.dq[:, 192 * b + 128:192 * b + 192], A.add))
-    c = tt(T.rt[:, 515:768:4], T.g3[:, 128:192], T.pd3[:, 128:192], A.add, c_g2)
+    c_b2 = book2(1)
+    cg = rest_gather(128, 192, T.l1[:, 8:12], c_l)
+    c_pl = ts(T.pl[:], T.psd[:, 0:12], 192.0, None, A.add, None, mp)
+    c = rest_add(128, 192, cg)
     c_r2 = quant(T.rcq[:], T.rcqs[:], T.rt[:, 256:768], c)
     ma = scores(0, "raq", 0, "b2q", c_r, c_l, c_b2)
-    mc = scores(1, "rcq", 0, "b2q", c_r2)
-    vs = pick_scales("vbq", 0, 192, "p1q", 128, T.l1[:, 0:12])
-    act(T.nbf[:, 0:4], T.n1a[:, 0:4], F.Copy)
-    act(T.nbf[:, 8:12], T.n1c[:, 4:8], F.Copy)
-    va, sa = words(0, ma, T.rm2, T.jk2, T.n2a)
-    vv = pick_codes("vbq", 0, 192, "p1q", 128, T.l1[:, 0:12])
-    vc, sc = words(1, mc, T.rm2, T.jk2, T.n2c)
+    mc = scores(2, "rcq", 0, "b2q", c_r2)
+
+    def part_v(k):
+        return pick_codes("vbq", 64 * k, 64 * k + 64, "p1q", 128, T.l1[:, 4 * k:4 * k + 4])
+    for k in range(3):
+        vs = pick_scales("vbq", 64 * k, 64 * k + 64, "p1q", 128, T.l1[:, 4 * k:4 * k + 4])
     fan_scales("vbq", "lvq", "vin", vs)
+    act(T.nbf[:, 0:4], T.nf[:, 0:4], F.Copy)
+    act(T.nbf[:, 8:12], T.nf[:, 20:24], F.Copy)
+    for h in range(4):
+        _, sa = word(0, h, ma, T.rm2, T.jk2, N2A)
+    for h in range(3):
+        word(2, h, mc, T.rm2, T.jk2, N2C)
+    c = part_hi(N2A, O0, "xa", 32, sa)
+    vc, sc = word(2, 3, mc, T.rm2, T.jk2, N2C)
+    c = part_lo(N2A, O0, "xa", 32, c)
+    part_v(0)
+    c = part_q("xa", c)
+    la = tolist(T.psa, "xa", 8, c)
+    c = part_hi(N2C, O1, "xc", 16, sc)
+    part_v(1)
+    c = part_lo(N2C, O1, "xc", 16, c)
+    vv = part_v(2)
+    c = part_q("xc", c)
+    lc = tolist(T.psb, "xc", 4, c)
     fan_codes("vbq", "lvq", "vin", vv)
     need("y", vv, vs)
     dma("y", T.lvq[:, 144:192].bitcast(dt.uint8), T.vbq[:, 144:192].bitcast(dt.uint8), "dv")
     dma("y", T.lvqs[:, 144:192], T.vbqs[:, 144:192], "dv")
-    la = tolist(T.psa, "xa", 8, spread(T.n2a, T.ofa[:, 0:2], "xa", 32, sa))
-    lc = tolist(T.psd, "xc", 4, spread(T.n2c, T.ofa[:, 2:3], "xc", 16, sc))
-    act(T.nbf[:, 4:8], T.n2a[:, 0:4], F.Copy, sc)
-    c_nb = act(T.nbf[:, 12:16], T.n2c[:, 4:8], F.Copy)
+    act(T.nbf[:, 4:8], T.nf[:, 32:36], F.Copy, sc)
+    c_nb = act(T.nbf[:, 12:16], T.nf[:, 52:56], F.Copy)
     fan([T.nbf[:, 8 * (a // 2):8 * (a // 2) + 8] for a in range(3)], [T.ln[:, 32 * (2 - a):32 * (2 - a) + 8] for a in range(3)], "nin", c_nb)
-    c_ln3 = act(T.ln[:, 96:104], T.nbf[:, 8:16], F.Copy, c_nb, c_ln)
-    c_l = ts(T.l2[:, 0:8], T.psa[:, 0:8], T.hcol[:], None, A.add, None, la, c_hc)
+    c_l = ts(T.l2[:, 0:8], T.psa[:, 0:8], T.hcol[:], None, A.add, None, la, c_hcol)
     pick("v2q", 0, 128, "b2q", 512, T.l2[:, 0:8], c_l)
-    c_l = ts(T.l2[:, 8:9], T.psd[:, 0:1], T.hcol[:], None, A.add, None, lc)
+    c_l = ts(T.l2[:, 8:9], T.psb[:, 0:1], T.hcol[:], None, A.add, None, lc)
+    c_l2 = ts(T.l2b[:, 0:3], T.psb[:, 1:4], T.hcol[:], None, A.add, None)
     wv, ws = pick("v2q", 128, 144, "b2q", 512, T.l2[:, 8:9], c_l)
     fan_codes("v2q", "lwq", "win", wv)
     fan_scales("v2q", "lwq", "win", ws)
-    c_l = ts(T.l2b[:, 0:3], T.psd[:, 1:4], T.hcol[:], None, A.add, None)
-    wo = pick("lwq", 144, 192, "b2q", 512, T.l2b[:, 0:3], c_l)
+    wo = pick("lwq", 144, 192, "b2q", 512, T.l2b[:, 0:3], c_l2)
+    c_ln3 = act(T.ln[:, 96:104], T.nbf[:, 8:16], F.Copy, c_nb, c_ln)
 
-    mp = tolist(T.psb, "xp", 12, spread(T.pf, T.ofa[:, 4:7], "xp", 48, c_pf))
     c_q = quant(T.wq[:], T.wqs[:], T.wb[:], ("dw", 16))
     c_wt = fill(T.wt[:], -1.0)
-    c_l = ts(T.pl[:], T.psb[:, 0:12], 192.0, None, A.add, None, mp)
-    ov, os_ = pick("o1q", 0, 192, "lvq", 208, T.pl[:, 0:12], c_l, ("vin", 2 * landing), ("dv", 32), ("dz", 64))
+    ov, os_ = pick("o1q", 0, 192, "lvq", 208, T.pl[:, 0:12], c_pl, ("vin", 2 * landing), ("dv", 32), ("dz", 64))
     need("y", ov, os_)
     dma("y", T.oc[:, 0:768], T.o1q[:].bitcast(dt.uint8), "st")
     for k in range(4):
         dma("y", T.osc[4 * k:4 * k + 4, 0:192], T.o1qs[32 * k:32 * k + 4, :], "st")
-    mm(T.psc[:, 0:208], "wq", 0, 128, "lvq", 0, 208, True, False, c_q, ("vin", 2 * landing), ("dv", 32), ("dz", 64))
-    m = mm(T.psc[:, 0:208], "wq", 0, 128, "lwq", 0, 208, False, True, ("win", 2 * landing), wo[0], wo[1])
+    mm(T.psc[:, 0:192], "wq", 0, 128, "o1q", 0, 192, True, False, c_q, ov, os_, vc)
     need("v", c_ln3, ("nin", landing))
     c = done("v", V.transpose(T.tr[:], T.ln[:]))
-    for a, q, i, n, o in ((0, 1, 0, 32, 0), (0, 2, 0, 16, 32), (1, 1, 16, 16, 0), (1, 2, 0, 32, 16), (2, 0, 0, 32, 0), (2, 1, 0, 16, 32), (3, 2, 16, 16, 0), (3, 3, 0, 32, 16)):
-        c_t = act(T.wt[0:32, 48 * a + o:48 * a + o + n], T.tr[32 * q:32 * q + 32, 32 * a + i:32 * a + i + n], F.Copy, c, c_wt)
-    need("v", c_t)
-    c = done("v", V.tensor_copy(T.wno[:], T.wt[:, 0:208].indirect(T.pl[:, 0:12])))
-    need("y", c)
-    dma("y", T.wn[:], T.wno[0:8, :], "st")
+    c_t = []
+    for k, (a, q, i, n, o) in enumerate(((0, 1, 0, 32, 0), (0, 2, 0, 16, 32), (1, 1, 16, 16, 0), (1, 2, 0, 32, 16),
+                                         (2, 0, 0, 32, 0), (2, 1, 0, 16, 32), (3, 2, 16, 16, 0), (3, 3, 0, 32, 16))):
+        out, in_ = T.wt[0:32, 48 * a + o:48 * a + o + n], T.tr[32 * q:32 * q + 32, 32 * a + i:32 * a + i + n]
+        c_t.append(act(out, in_, F.Copy, c, c_wt) if k % 2 else copy(out, in_, c, c_wt))
     ov, os_ = pick("o2q", 0, 192, "lwq", 208, T.pl[:, 0:12], ("win", 2 * landing), wo[0], wo[1])
+    m = mm(T.psc[:, 0:192], "wq", 0, 128, "o2q", 0, 192, False, True, ov, os_)
     need("y", ov)
     dma("y", T.oc[:, 768:1536], T.o2q[:].bitcast(dt.uint8), "st")
     need("s", os_)
     for k in range(4):
         dma("s", T.osc[4 * k:4 * k + 4, 192:384], T.o2qs[32 * k:32 * k + 4, :], "st")
-    c = copy(T.ysl[:], T.psc[:, 0:208], m)
-    need("v", c)
-    c = done("v", V.tensor_copy(T.ysb[:], T.ysl[:].indirect(T.pl[:, 0:12])))
+    need("v", *c_t)
+    c_n = done("v", V.tensor_copy(T.wno[:], T.wt[:, 0:208].indirect(T.pl[:, 0:12])))
+    c = copy(T.ysb[:], T.psc[:, 0:192], m)
+    need("y", c_n)
+    dma("y", T.wn[:], T.wno[0:8, :], "st")
     need("y", c)
     dma("y", T.y[:], T.ysb[:], "st")
 

from concourse.bass import DstId, RemoteDMATransfer
from concourse.mybir import dt, AluOpType, AxisListType, ActivationFunctionType

A = AluOpType
F = ActivationFunctionType
NR = 4
LOW = -1e29
RND = 1.5 * 2.0 ** 27


def _codes(n):
    return ("sbuf", [128, n], "float8_e4m3fn_x4")


def _plane(n):
    return ("sbuf", [128, n], "uint8")


def _sb(n, d):
    return ("sbuf", [128, n], d)


SCRATCH = {}
for _n, _w in (("xq", 192), ("cq", 134), ("wq", 128), ("p1q", 128), ("b1q", 512), ("b2q", 512), ("trq", 256), ("wlq", 128), ("epq", 512),
               ("otq", 134), ("abq", 140), ("xaq", 136), ("xcq", 132), ("xpq", 140), ("zsq", 144), ("zq", 192), ("vbq", 192), ("lvq", 208),
               ("v2q", 144), ("lwq", 208), ("raq", 128), ("rcq", 128), ("o1q", 192), ("o2q", 192)):
    SCRATCH[_n] = _codes(_w)
    SCRATCH[_n + "s"] = _plane(_w)
for _n, _w in (("xb", 768), ("cb", 536), ("wb", 512), ("pb1", 512), ("pb2", 512), ("bm1", 2048), ("bm2", 2048), ("trb", 516), ("wlb", 512),
               ("epb", 516), ("ot", 536), ("ab", 560), ("xa", 544), ("xc", 528), ("xp", 560), ("rt", 768), ("zz", 536), ("on1", 128),
               ("t1", 128), ("im", 128), ("jk1", 1024), ("jk2", 1024), ("nbf", 16), ("ln", 128), ("tr", 128)):
    SCRATCH[_n] = _sb(_w, "bfloat16")
for _n, _w in (("rst", 10), ("rma", 10), ("ua", 11), ("rr", 10), ("hc", 2), ("nl", 2), ("tk", 4), ("tkn", 2), ("ib", 12), ("abx", 12),
               ("vl", 1), ("mk", 4), ("hcol", 1), ("df", 1), ("e0", 1), ("e4", 1), ("off", 2), ("rm1", 1024), ("rm2", 1024), ("nf", 80),
               ("tf", 2), ("q1", 2), ("wt", 208), ("wno", 192), ("ysb", 192), ("db", 512), ("dq", 384), ("g2", 192), ("g3", 192)):
    SCRATCH[_n] = _sb(_w, "float32")
for _n, _w in (("pi", 1), ("pa", 1), ("pb", 1), ("gi", 1), ("ui", 1), ("ti", 1), ("hi", 1), ("vi", 2), ("ai", 2), ("bi", 2)):
    SCRATCH[_n] = _sb(_w, "int32")
for _n, _w in (("zl", 12), ("zl2", 4), ("pl", 12), ("l1", 12), ("l2", 12), ("l2b", 4), ("ofo", 2), ("ofa", 8)):
    SCRATCH[_n] = _sb(_w, "uint16")
for _n in ("psa", "psb", "psc", "psd", "pd0", "pd1", "pd2", "pd3"):
    SCRATCH[_n] = ("psum", [128, 512], "float32")
SEMAPHORES = ["qv", "qs", "qt", "qg", "dx", "dco", "dp1", "dp2", "db2", "dep", "dw", "dz", "dv", "do", "st", "zin", "vin", "win", "nin", "oin",
              "left"]


def _mask(topo, src, peers):
    out, far, near = {}, 0, 0
    for c in peers:
        e = topo.engines(src, c)
        if topo.die(src) != topo.die(c):
            out[c] = e[far * 8:far * 8 + 8:2]
            far += 1
        else:
            out[c] = e[1 + near * 8:9 + near * 8:2]
            near += 1
    return out


def rank_program(g, core, T, topo):
    rank = T.rank_of(core)
    if rank is None:
        return
    S = T.sem
    eng = {"v": g.vector, "s": g.scalar, "t": g.tensor, "g": g, "y": g.sync}
    qsem = {"v": "qv", "s": "qs", "t": "qt", "g": "qg"}
    cnt = {"v": 0, "s": 0, "t": 0, "g": 0}
    seen = {q: {} for q in eng}

    def need(q, *deps):
        for sem, val in deps:
            if seen[q].get(sem, 0) < val:
                eng[q].wait_ge(S[sem], val)
                seen[q][sem] = val

    def done(q, ins):
        ins.then_inc(S[qsem[q]], 1)
        cnt[q] += 1
        return (qsem[q], cnt[q])

    V, SC, TE = g.vector, g.scalar, g.tensor
    stores = [0]

    def dma(q, out, in_, sem):
        eng[q].dma_start(out, in_).then_inc(S[sem], 16)
        if sem == "st":
            stores[0] += 1

    def ts(out, in0, s1, s2, op0, op1, *deps):
        need("v", *deps)
        if op1 is None:
            return done("v", V.tensor_scalar(out, in0, s1, s2, op0))
        return done("v", V.tensor_scalar(out, in0, s1, s2, op0, op1))

    def tt(out, a, b, op, *deps):
        need("v", *deps)
        return done("v", V.tensor_tensor(out, a, b, op))

    def fill(ap, c, *deps):
        need("v", *deps)
        return done("v", V.memset(ap, c))

    def copy(out, in_, *deps):
        need("v", *deps)
        return done("v", V.tensor_copy(out, in_))

    def quant(q, s, in_, *deps):
        need("v", *deps)
        return done("v", V.quantize_mx(q, s, in_))

    def act(out, in_, func, *deps):
        need("s", *deps)
        return done("s", SC.activation(out, in_, func))

    def mm(out, name, c0, c1, mov, m0, m1, start, stop, *deps):
        need("t", *deps)
        return done("t", TE.matmul_mx(out, T[name][:, c0:c1], T[name + "s"][:, c0:c1], T[mov][:, m0:m1], T[mov + "s"][:, m0:m1], start, stop))

    def pick_codes(dst, d0, d1, win, w1, lst, *deps):
        need("v", *deps)
        return done("v", V.tensor_copy(T[dst][:, d0:d1].bitcast(dt.uint32), T[win][:, 0:w1].bitcast(dt.uint32).indirect(lst)))

    def pick_scales(dst, d0, d1, win, w1, lst, *deps):
        return act(T[dst + "s"][:, d0:d1], T[win + "s"][:, 0:w1].indirect(lst), F.Copy, *deps)

    def pick(*a):
        return pick_codes(*a), pick_scales(*a)

    peers = [T.cores[(rank + 1 + a) % NR] for a in range(3)]
    emask = _mask(topo, core, peers)
    landing = sum(len(_mask(topo, c, [T.cores[(T.rank_of(c) + 1 + a) % NR] for a in range(3)])[core]) for c in peers)
    left = [0]

    def fan(srcs, dsts, sem, *deps):
        need("g", *deps)
        tr = []
        for a, c in enumerate(peers):
            rid, pid, _ = topo.addr(c)
            tr.append(RemoteDMATransfer(dst_ids=[DstId(rid=rid, pnc=pid)], dma_engine_mask=sum(1 << e for e in emask[c]),
                                        remote_sem=S[sem], srcs=[srcs[a]], dsts=[dsts[a]]))
            left[0] += len(emask[c])
        g.remote_dma_fused(tr, local_sem=S["left"])

    def fan_codes(src, dst, sem, *c):
        fan([T[src][:, 48 * a:48 * a + 48].bitcast(dt.uint8) for a in range(3)],
            [T[dst][:, 48 * (2 - a):48 * (2 - a) + 48].bitcast(dt.uint8) for a in range(3)], sem, *c)

    def fan_scales(src, dst, sem, *c):
        fan([T[src + "s"][:, 48 * a:48 * a + 48] for a in range(3)], [T[dst + "s"][:, 48 * (2 - a):48 * (2 - a) + 48] for a in range(3)], sem, *c)

    dma("y", T.xb[:], T.x[:], "dx")
    dma("s", T.cb[:, 24:40], T.co[:, 0:4 * NR], "dco")
    dma("y", T.pb1[:], T.b1[:], "dp1")

    c_pi = done("g", g.iota(T.pi[:], [[0, 1]], 0, 1))
    c_on = fill(T.on1[:], 1.0)
    c_zz = fill(T.zz[:], 0.0)
    need("y", c_zz)
    dma("y", T.epb[:], T.zz[:, 0:516], "dep")
    dma("y", T.pb2[:], T.b2[:], "dp2")
    need("s", c_zz)
    c_tr = done("s", SC.activation(T.trb[:], T.zz[:, 0:516], F.Identity, bias=1.0))
    c_ot = act(T.ot[:], T.zz[:], F.Copy)
    need("g", c_on)
    c_t1 = done("g", g.affine_select(T.t1[:], T.on1[:], [[1, 128]], A.is_gt, 0.0, 0, -1))
    c_cb = done("g", g.iota(T.cb[:, 40:536], [[0, 496]], 0, 0, allow_small_or_imprecise_dtypes=True))
    ts(T.gi[:], T.pi[:], 4, None, A.arith_shift_right, None, c_pi)
    c = ts(T.ui[:], T.pi[:], 2, 3, A.arith_shift_right, A.bitwise_and)
    ts(T.ti[:], T.pi[:], 3 if rank < 2 else 0, None, A.bitwise_and, None)
    c_hi = ts(T.hi[:], T.pi[:], 5, None, A.arith_shift_right, None)
    c = tt(T.df[:], T.gi[:], T.ui[:], A.subtract, c)
    c_cb0 = fill(T.cb[:, 0:24], 0.0)
    for h in range(4):
        c_mk = ts(T.mk[:, h:h + 1], T.hi[:], float(h), None, A.is_equal, None, c_hi)
    if rank % 2 == 0:
        ts(T.e0[:], T.df[:], 0.0, None, A.is_equal, None, c)
    c = ts(T.e4[:], T.df[:], 4.0, None, A.is_equal, None, c)
    c_tr = fill(T.trb[:, 2:516:4], 0.0, c_tr)
    for k, (e, v) in enumerate((((T.e0, -8.0), (T.e4, -8.0)), ((T.e4, -4.0),))[rank % 2]):
        c = ts(T.off[:, k:k + 1], T.ti[:], v, e[:], A.add, A.mult, c)
    wide = 2 - rank % 2
    c_rs = fill(T.rst[:], 0.0)
    c_of = ts(T.ofo[:, 0:wide], T.off[:, 0:wide], 8.0, None, A.add, None, c)
    c_rs = fill(T.rst[:, 4:7], LOW, c_rs)
    need("g", c_t1, c_tr)
    c_tri = done("g", g.affine_select(T.trb[:, 1:513:4], T.t1[:], [[1, 128]], A.not_equal, 1024.0, 0, -1))
    need("g", c_ot)
    c_oi = done("g", g.iota(T.ot[:, 27:75:4], [[0, 2], [2, 6]], 0, 0, allow_small_or_imprecise_dtypes=True))
    own = slice(2 * rank, 2 * rank + wide)
    fan([T.ofo[:, 0:wide]] * 3, [T.ofa[:, own]] * 3, "oin", c_of)
    need("y", c_of)
    dma("y", T.ofa[:, own], T.ofo[:, 0:wide], "do")
    if rank < NR - 1:
        done("g", g.iota(T.ib[:, 0:9 - 3 * rank], [[256, 3 - rank], [16, 3]], 1280 + 256 * rank, 0, allow_small_or_imprecise_dtypes=True))
    c_ib = done("g", g.iota(T.ib[:, 9 - 3 * rank:12], [[256, rank + 1], [16, 3]], 1024, 0, allow_small_or_imprecise_dtypes=True))
    c_im = done("g", g.iota(T.im[:], [[0, 8], [1, 16]], 0, 0, allow_small_or_imprecise_dtypes=True))
    need("g", ("dep", 16))
    c_ep = done("g", g.affine_select(T.epb[:, 4:516:4], T.on1[:], [[1, 128]], A.is_equal, 0.0, 0, -1))
    c_w0 = act(T.wlb[:], T.zz[:, 0:512], F.Copy)
    c_xp = act(T.xp[:, 96:560], T.zz[:, 0:464], F.Copy)

    def masked(bm, pb, h):
        return done("s", SC.activation(bm[:, 512 * h:512 * h + 512], pb[:], F.Copy, scale=T.mk[:, h:h + 1]))
    need("s", c_mk, ("dp1", 16))
    for h in range(3):
        masked(T.bm1, T.pb1, h)

    c_q = quant(T.cq[:], T.cqs[:], T.cb[:], ("dco", 16), c_cb, c_cb0)
    c_x = quant(T.xq[:], T.xqs[:], T.xb[:], ("dx", 16))
    need("y", c_q)
    for b in ("lvq", "lwq"):
        dma("y", T[b][:, 192:208].bitcast(dt.uint8), T.cq[:, 64:80].bitcast(dt.uint8), "dz")
        dma("y", T[b + "s"][:, 192:208], T.cqs[:, 64:80], "dz")
    mm(T.psa[:, 0:128], "xq", 0, 128, "cq", 6, 134, True, False, c_x)
    m = mm(T.psa[:, 0:128], "xq", 64, 192, "cq", 0, 128, False, True)
    c_ua = fill(T.ua[:], 0.0)
    c_vl = ts(T.vl[:], T.pi[:], 64.0, None, A.is_ge, None)
    c_o1 = fill(T.ot[:, 1:64:4], -7.5 / 128, c_ot)
    for k in range(2):
        quant(T.trq[:, 128 * k:128 * k + 128], T.trqs[:, 128 * k:128 * k + 128], T.trb[:, 1 + 2 * k:513 + 2 * k], c_tri)

    def scan(out, d0, d1, *deps):
        need("v", *deps)
        return done("v", V.tensor_tensor_scan(out, d0, d1, LOW, A.add, A.max))
    s = scan(T.rma[:], T.rst[:], T.psa[:, 0:10], m, c_rs)
    ts(T.pa[:], T.pi[:], 112, None, A.bitwise_and, None)
    u = ts(T.ua[:, 1:5], T.rma[:, 0:4], T.rma[:, 3:4], None, A.is_equal, None, s, c_ua)
    u = ts(T.ua[:, 7:11], T.rma[:, 6:10], T.rma[:, 9:10], T.vl[:], A.is_equal, A.mult, c_vl)
    c_pb = ts(T.pb[:], T.pi[:], 15, None, A.bitwise_and, None)
    o = tt(T.ot[:, 24:64:4], T.ua[:, 1:11], T.ua[:, 0:10], A.subtract, u, c_o1)
    c_o = quant(T.otq[:], T.otqs[:], T.ot[:], o, c_oi)
    mm(T.psc[:, 0:128], "trq", 0, 128, "otq", 6, 134, True, False, c_o)
    m = mm(T.psc[:, 0:128], "trq", 128, 256, "otq", 0, 128, False, True)
    ts(T.tk[:, 2:3], T.pa[:], 64.0, T.vl[:], A.add, A.mult, c_pb)
    c = ts(T.tk[:, 3:4], T.pb[:], T.vl[:], None, A.mult, None)
    copy(T.tk[:, 0:1], T.pa[:])
    c_tk = copy(T.tk[:, 1:2], T.pb[:])
    c_tn = ts(T.tkn[:], T.tk[:, 2:4], -0.0625, None, A.mult, None, c)
    c_ln = fill(T.ln[:], 0.0)
    r = scan(T.rr[:], T.rst[:], T.psc[:, 0:10], m)
    c_hc = ts(T.hc[:], T.rr[:, 3:10:6], RND, RND, A.add, A.subtract, r)
    need("s", c_hc, c_ib, c_tn)
    c = done("s", SC.activation(T.abx[:], T.ib[:], F.Abs, bias=T.hc[:, 1:2], scale=-1.0))
    need("s", c)
    for t in (2, 3):
        c_b = done("s", SC.activation(T.ab[:, 512 + t:560:4], T.abx[:], F.Relu, bias=T.tk[:, t:t + 1], scale=T.tkn[:, t - 2:t - 1]))
    c_m1 = masked(T.bm1, T.pb1, 3)
    c_nl = tt(T.nl[:], T.hc[:], T.rr[:, 3:10:6], A.subtract, c_hc)
    for t in range(2):
        ts(T.ab[:, 512 + t:560:4], T.ib[:], T.hc[:, 0:1], T.tk[:, t:t + 1], A.is_equal, A.mult, c_tk, c_ib)
    for t in range(4):
        c_a = ts(T.ab[:, t:512:4], T.im[:], T.nl[:, t // 2:t // 2 + 1], 7.5, A.subtract, A.is_equal, c_nl, c_im) if False else \
            ts(T.ab[:, t:512:4], T.im[:], T.nl[:, t // 2:t // 2 + 1], 7.5, A.add, A.is_equal, c_nl, c_im)
    c_a = quant(T.abq[:], T.abqs[:], T.ab[:], c_a, c_b)
    m0 = mm(T.psa[:, 0:128], "abq", 0, 128, "abq", 12, 140, True, True, c_a)

    def e_tile(b):
        return quant(T.epq[:, 128 * b:128 * b + 128], T.epqs[:, 128 * b:128 * b + 128], T.epb[:, 4 - b:516 - b], c_ep)
    c_e = [e_tile(0), e_tile(1)]
    c_l = copy(T.zl[:, 0:9], T.psa[:, 116:125], m0)
    zv, zs = pick("zsq", 0, 144, "xq", 192, T.zl[:, 0:9], c_l)
    fan_codes("zsq", "zq", "zin", zv, c_ln)
    fan_scales("zsq", "zq", "zin", zs)
    c_l = copy(T.zl2[:, 0:3], T.psa[:, 125:128])
    c_p1 = quant(T.p1q[:], T.p1qs[:], T.pb1[:], ("dp1", 16))
    zo = pick("zq", 144, 192, "xq", 192, T.zl2[:, 0:3], c_l)

    c_xc = done("g", g.iota(T.xc[:, 32:528], [[0, 496]], 0, 0, allow_small_or_imprecise_dtypes=True))
    for h in range(2):
        c_g = done("g", g.iota(T.bm2[:, 512 * h:512 * h + 512], [[0, 512]], 0, 0, allow_small_or_imprecise_dtypes=True))
    need("y", c_g)
    for h in range(2):
        dma("y", T.bm2[32 * h:32 * h + 32, 512 * h:512 * h + 512], T.b2[32 * h:32 * h + 32, :], "db2")
    dma("y", T.wb[:], T.w[:], "dw")
    c_db = []

    def table(b):
        m = mm(T["pd%d" % b][:, 0:128], "epq", 128 * b, 128 * b + 128, "p1q", 0, 128, True, True, c_e[b], c_p1)
        need("s", m)
        c_db.append(done("s", SC.activation(T.db[:, 128 * b:128 * b + 128], T["pd%d" % b][:, 0:128], F.Copy, scale=-1.0)))
    table(0)
    table(1)
    c_xa = act(T.xa[:, 64:544], T.zz[:, 0:480], F.Copy)
    c_e.append(e_tile(2))
    c_e.append(e_tile(3))
    table(2)
    table(3)
    c_b1 = quant(T.b1q[:], T.b1qs[:], T.bm1[:], c_m1)
    need("s", ("dp2", 16))
    for h in (2, 3):
        c_m2 = masked(T.bm2, T.pb2, h)
    c_f = fill(T.nf[:], 0.0)
    for t in range(4):
        c_w = ts(T.wlb[:, 129 * t:128 * t + 128:4], T.im[:, 0:32], T.tk[:, 1:2], None, A.is_equal, None, c_w0)
    c = ts(T.vi[:], T.rr[:, 3:10:6], -1016.5 + 256 * (3 - rank), None, A.add, None)
    c_w = quant(T.wlq[:], T.wlqs[:], T.wlb[:], c_w)
    ts(T.ai[:], T.vi[:], 8, 3, A.arith_shift_right, A.bitwise_and, c)
    c_bi = ts(T.bi[:], T.vi[:], 255, None, A.bitwise_and, None)
    c_hcol = ts(T.hcol[:], T.hi[:], 128.0, None, A.mult, None)

    where = ((("psa", 0), ("psb", 0), ("psc", 0), ("psc", 128)), (("psd", 0), ("psd", 128), ("psd", 256), ("psd", 384)),
             (("pd0", 0), ("pd1", 0), ("pd2", 0), ("pd3", 0)))
    N1A, N1C, N2A, N2C, NP = 0, 16, 32, 48, 64
    O0, O1, OP = T.ofa[:, 0:2], T.ofa[:, 2:3], T.ofa[:, 4:7]

    def scores(k, tok, c0, bk, *deps):
        if k == 2:
            return [mm(T["pd%d" % h][:, 0:128], tok, c0, c0 + 128, bk, 128 * h, 128 * h + 128, True, True, *deps) for h in range(4)]
        if k == 1:
            return [mm(T.psd[:, 0:512], tok, c0, c0 + 128, bk, 0, 512, True, True, *deps)] * 4
        m = [mm(T[("psa", "psb")[h]][:, 0:128], tok, c0, c0 + 128, bk, 128 * h, 128 * h + 128, True, True, *deps) for h in range(2)]
        return m + [mm(T.psc[:, 0:256], tok, c0, c0 + 128, bk, 256, 512, True, True)] * 2

    def word(k, h, m, rm, jk, at):
        s = min(k, 1)
        e = 512 * s + 128 * h
        b, o = where[k][h]
        cv = scan(rm[:, e:e + 128], T.zz[:, 0:128], T[b][:, o:o + 128], m[h])
        need("s", cv, c_f)
        return cv, done("s", SC.activation(jk[:, e:e + 128], rm[:, e:e + 128], F.Sign, bias=rm[:, e + 127:e + 128], scale=-1.0,
                                           accum_out=T.nf[:, at + 4 * s + h:at + 4 * s + h + 1]))

    def part_hi(at, off, xt, n, *deps):
        need("v", *deps)
        return done("v", V.tensor_scalar(T[xt][:, 0:n], T.nf[:, at:at + 16].indirect(off), RND, RND, A.add, A.subtract))

    def part_lo(at, off, xt, n, c):
        need("v", c)
        return done("v", V.tensor_tensor(T[xt][:, n:2 * n], T.nf[:, at:at + 16].indirect(off), T[xt][:, 0:n], A.subtract))

    def part_q(xt, c):
        return quant(T[xt + "q"][:], T[xt + "qs"][:], T[xt][:], c)

    def tolist(bank, xt, w, *deps):
        mm(bank[:, 0:128], "wlq", 0, 128, xt + "q", 0, 128, True, False, *deps)
        return mm(bank[:, 0:128], "wlq", 0, 128, xt + "q", w, 128 + w, False, True)

    def book2(h, *deps):
        return quant(T.b2q[:, 128 * h:128 * h + 128], T.b2qs[:, 128 * h:128 * h + 128], T.bm2[:, 512 * h:512 * h + 512], *deps)

    def unpack(b):
        return mm(T["pd%d" % b][:, 0:192], "epq", 128 * b, 128 * b + 128, "zq", 0, 192, True, True, c_db[b])

    ma = scores(0, "zq", 0, "b1q", ("zin", 2 * landing), zo[0], zo[1], c_b1)
    mc = scores(1, "zq", 64, "b1q")
    md = [unpack(b) for b in range(4)]
    word(0, 0, ma, T.rm1, T.jk1, N1A)
    cq1 = ts(T.q1[:], T.ai[:], 48.0, -192.0, A.mult, A.add, c_bi)
    word(0, 1, ma, T.rm1, T.jk1, N1A)
    ts(T.tf[:], T.bi[:], 48.0, None, A.is_lt, None)
    cq1 = tt(T.q1[:], T.q1[:], T.bi[:], A.add, cq1)
    word(0, 2, ma, T.rm1, T.jk1, N1A)
    c_pf = tt(T.nf[:, 64:72:4], T.q1[:], T.tf[:], A.mult, cq1, c_f)
    _, sa = word(0, 3, ma, T.rm1, T.jk1, N1A)
    cx = part_hi(NP, OP, "xp", 48, c_pf, c_xp, ("oin", landing), ("do", 16))
    word(1, 0, mc, T.rm1, T.jk1, N1C)
    cx = part_lo(NP, OP, "xp", 48, cx)
    word(1, 1, mc, T.rm1, T.jk1, N1C)
    c = part_hi(N1A, O0, "xa", 32, sa, c_xa)
    word(1, 2, mc, T.rm1, T.jk1, N1C)
    c = part_lo(N1A, O0, "xa", 32, c)
    _, sc = word(1, 3, mc, T.rm1, T.jk1, N1C)
    c = part_q("xa", c)
    la = tolist(T.psa, "xa", 8, c, c_w)
    cx = part_q("xp", cx)
    c = part_hi(N1C, O1, "xc", 16, sc, c_xc)
    book2(2, c_m2)
    c = part_lo(N1C, O1, "xc", 16, c)
    book2(3)
    c = part_q("xc", c)
    lc = tolist(T.psb, "xc", 4, c)
    mp = tolist(T.psd, "xp", 12, cx)
    c_d = [act(T.dq[:, 192 * b:192 * b + 192], T["pd%d" % b][:, 0:192], F.Copy, md[b]) for b in range(2)]

    def rest_gather(d0, d1, lst, c):
        need("v", c)
        for b in range(2):
            need("v", c_d[b])
            done("v", V.tensor_tensor(T.rt[:, 4 * d0 + b:4 * d1:4], T.db[:, 128 * b:128 * b + 128].indirect(lst), T.dq[:, 192 * b + d0:192 * b + d1], A.add))
        return [act(T["g%d" % b][:, d0:d1], T.db[:, 128 * b:128 * b + 128].indirect(lst), F.Copy, c) for b in (2, 3)]

    def rest_add(d0, d1, cg):
        for b in (2, 3):
            c = tt(T.rt[:, 4 * d0 + b:4 * d1:4], T["g%d" % b][:, d0:d1], T["pd%d" % b][:, d0:d1], A.add, cg[b - 2], md[b])
        return c
    c_l = copy(T.l1[:, 0:8], T.psa[:, 0:8], la)
    cg = rest_gather(0, 128, T.l1[:, 0:8], c_l)
    c_l = copy(T.l1[:, 8:12], T.psb[:, 0:4], lc)
    book2(0, ("db2", 32))
    c = rest_add(0, 128, cg)
    c_r = quant(T.raq[:], T.raqs[:], T.rt[:, 0:512], c)
    c_b2 = book2(1)
    cg = rest_gather(128, 192, T.l1[:, 8:12], c_l)
    c_pl = ts(T.pl[:], T.psd[:, 0:12], 192.0, None, A.add, None, mp)
    c = rest_add(128, 192, cg)
    c_r2 = quant(T.rcq[:], T.rcqs[:], T.rt[:, 256:768], c)
    ma = scores(0, "raq", 0, "b2q", c_r, c_l, c_b2)
    mc = scores(2, "rcq", 0, "b2q", c_r2)

    def part_v(k):
        return pick_codes("vbq", 64 * k, 64 * k + 64, "p1q", 128, T.l1[:, 4 * k:4 * k + 4])
    for k in range(3):
        vs = pick_scales("vbq", 64 * k, 64 * k + 64, "p1q", 128, T.l1[:, 4 * k:4 * k + 4])
    fan_scales("vbq", "lvq", "vin", vs)
    act(T.nbf[:, 0:4], T.nf[:, 0:4], F.Copy)
    act(T.nbf[:, 8:12], T.nf[:, 20:24], F.Copy)
    for h in range(4):
        _, sa = word(0, h, ma, T.rm2, T.jk2, N2A)
    for h in range(3):
        word(2, h, mc, T.rm2, T.jk2, N2C)
    c = part_hi(N2A, O0, "xa", 32, sa)
    vc, sc = word(2, 3, mc, T.rm2, T.jk2, N2C)
    c = part_lo(N2A, O0, "xa", 32, c)
    part_v(0)
    c = part_q("xa", c)
    la = tolist(T.psa, "xa", 8, c)
    c = part_hi(N2C, O1, "xc", 16, sc)
    part_v(1)
    c = part_lo(N2C, O1, "xc", 16, c)
    vv = part_v(2)
    c = part_q("xc", c)
    lc = tolist(T.psb, "xc", 4, c)
    fan_codes("vbq", "lvq", "vin", vv)
    need("y", vv, vs)
    dma("y", T.lvq[:, 144:192].bitcast(dt.uint8), T.vbq[:, 144:192].bitcast(dt.uint8), "dv")
    dma("y", T.lvqs[:, 144:192], T.vbqs[:, 144:192], "dv")
    act(T.nbf[:, 4:8], T.nf[:, 32:36], F.Copy, sc)
    c_nb = act(T.nbf[:, 12:16], T.nf[:, 52:56], F.Copy)
    fan([T.nbf[:, 8 * (a // 2):8 * (a // 2) + 8] for a in range(3)], [T.ln[:, 32 * (2 - a):32 * (2 - a) + 8] for a in range(3)], "nin", c_nb)
    c_l = ts(T.l2[:, 0:8], T.psa[:, 0:8], T.hcol[:], None, A.add, None, la, c_hcol)
    pick("v2q", 0, 128, "b2q", 512, T.l2[:, 0:8], c_l)
    c_l = ts(T.l2[:, 8:9], T.psb[:, 0:1], T.hcol[:], None, A.add, None, lc)
    c_l2 = ts(T.l2b[:, 0:3], T.psb[:, 1:4], T.hcol[:], None, A.add, None)
    wv, ws = pick("v2q", 128, 144, "b2q", 512, T.l2[:, 8:9], c_l)
    fan_codes("v2q", "lwq", "win", wv)
    fan_scales("v2q", "lwq", "win", ws)
    wo = pick("lwq", 144, 192, "b2q", 512, T.l2b[:, 0:3], c_l2)
    c_ln3 = act(T.ln[:, 96:104], T.nbf[:, 8:16], F.Copy, c_nb, c_ln)

    c_q = quant(T.wq[:], T.wqs[:], T.wb[:], ("dw", 16))
    c_wt = fill(T.wt[:], -1.0)
    ov, os_ = pick("o1q", 0, 192, "lvq", 208, T.pl[:, 0:12], c_pl, ("vin", 2 * landing), ("dv", 32), ("dz", 64))
    need("y", ov, os_)
    dma("y", T.oc[:, 0:768], T.o1q[:].bitcast(dt.uint8), "st")
    for k in range(4):
        dma("y", T.osc[4 * k:4 * k + 4, 0:192], T.o1qs[32 * k:32 * k + 4, :], "st")
    mm(T.psc[:, 0:192], "wq", 0, 128, "o1q", 0, 192, True, False, c_q, ov, os_, vc)
    need("v", c_ln3, ("nin", landing))
    c = done("v", V.transpose(T.tr[:], T.ln[:]))
    c_t = []
    for k, (a, q, i, n, o) in enumerate(((0, 1, 0, 32, 0), (0, 2, 0, 16, 32), (1, 1, 16, 16, 0), (1, 2, 0, 32, 16),
                                         (2, 0, 0, 32, 0), (2, 1, 0, 16, 32), (3, 2, 16, 16, 0), (3, 3, 0, 32, 16))):
        out, in_ = T.wt[0:32, 48 * a + o:48 * a + o + n], T.tr[32 * q:32 * q + 32, 32 * a + i:32 * a + i + n]
        c_t.append(act(out, in_, F.Copy, c, c_wt) if k % 2 else copy(out, in_, c, c_wt))
    ov, os_ = pick("o2q", 0, 192, "lwq", 208, T.pl[:, 0:12], ("win", 2 * landing), wo[0], wo[1])
    m = mm(T.psc[:, 0:192], "wq", 0, 128, "o2q", 0, 192, False, True, ov, os_)
    need("y", ov)
    dma("y", T.oc[:, 768:1536], T.o2q[:].bitcast(dt.uint8), "st")
    need("s", os_)
    for k in range(4):
        dma("s", T.osc[4 * k:4 * k + 4, 192:384], T.o2qs[32 * k:32 * k + 4, :], "st")
    need("v", *c_t)
    c_n = done("v", V.tensor_copy(T.wno[:], T.wt[:, 0:208].indirect(T.pl[:, 0:12])))
    c = copy(T.ysb[:], T.psc[:, 0:192], m)
    need("y", c_n)
    dma("y", T.wn[:], T.wno[0:8, :], "st")
    need("y", c)
    dma("y", T.y[:], T.ysb[:], "st")

    need("y", *[(qsem[q], cnt[q]) for q in cnt])
    need("y", ("st", 16 * stores[0]))
    need("g", ("left", left[0]))
